import numpy as np
import ml_dtypes


def mxq(x, axis, fmt="e4m3"):
    dtype, down = {"e4m3": (ml_dtypes.float8_e4m3fn, 7), "e5m2": (ml_dtypes.float8_e5m2, 14)}[fmt]
    v = np.moveaxis(np.asarray(x, np.float32).astype(ml_dtypes.bfloat16).astype(np.float64), axis, -1)
    blocks = v.reshape(v.shape[:-1] + (-1, 32))
    amax = np.abs(blocks).max(-1, keepdims=True)
    byte = np.maximum(np.where(amax > 0, np.frexp(amax)[1] - 1 + 127, 0) - down, 1)
    scale = np.exp2(byte - 127.0)
    codes = (blocks / scale).astype(np.float32).astype(dtype).astype(np.float64)
    return np.moveaxis((codes * scale).reshape(v.shape), -1, axis)


WIDE = False


def mx_kscale(k):
    if not WIDE:
        return np.ones(k)
    levels = np.array([10, -10, 5, -5, 0])
    if k % 512:
        return np.exp2(np.random.permutation(np.resize(levels, k // 32))).repeat(32)
    a = np.empty((k // 512, 16))
    for p in range(k // 512):
        a[p, :8] = np.random.permutation(np.resize(levels, 8))
        for g in range(8):
            far = levels[np.abs(levels - a[p, g]) >= 10]
            a[p, g + 8] = far[np.random.randint(len(far))]
    return np.exp2(a.ravel()).repeat(32)


def f64(x):
    return np.asarray(x).astype(np.float64)


def striped(idx):
    return np.tile(idx.reshape(-1, 16).T, (8, 1)).astype(np.uint16)


def unstriped(offs):
    return offs[:16].T.reshape(-1).astype(np.int64)


def pack_weight(w):
    k, n = w.shape
    w = f64(np.asarray(w, np.float32).astype(ml_dtypes.bfloat16)).reshape(k // 32, 32, n)
    amax = np.abs(w).max(1)
    byte = np.clip(np.where(amax > 0, np.frexp(amax)[1] - 1 + 127 - 7, 1), 1, 254)
    scaled = (w * np.exp2(127.0 - byte)[:, None, :]).reshape(k, n).astype(np.float32)
    words = np.ascontiguousarray(scaled.reshape(k // 512, 128, 4, n).transpose(0, 1, 3, 2)).astype(ml_dtypes.float8_e4m3fn).view(np.uint8)
    return words, np.ascontiguousarray(byte.astype(np.uint8).reshape(k // 512, 16, n))


def unpack_weight(words, scales):
    g, p, n, _ = words.shape
    vals = np.ascontiguousarray(words).view(ml_dtypes.float8_e4m3fn).astype(np.float64) * np.repeat(np.exp2(scales.astype(np.float64) - 127.0), 8, axis=1)[..., None]
    return vals.transpose(0, 1, 3, 2).reshape(g * 512, n)


def planes(y):
    n, m = y.shape
    v = y.astype(np.float32).astype(ml_dtypes.bfloat16).astype(np.float64).reshape(n // 32, 32, m)
    top = np.abs(v).max(1)
    byte = np.clip(np.where(top > 0, np.frexp(top)[1] - 1 + 127 - 7, 1), 1, 254)
    codes = (v * np.exp2(127.0 - byte)[:, None, :]).reshape(n, m).astype(np.float32).astype(ml_dtypes.float8_e4m3fn).view(np.uint8)
    words = codes.reshape(n // 512, 128, 4, m).transpose(0, 1, 3, 2)
    return np.ascontiguousarray(words), np.ascontiguousarray(byte.astype(np.uint8).reshape(n // 512, 16, m))


def sigmoid(v):
    return 1.0 / (1.0 + np.exp(-np.maximum(v, -700.0)))


K, T, S, N, W = 512, 1024, 512, 512, 2048


def setup_inputs():
    n = np.random.standard_normal
    s = mx_kscale(K)[:, None]
    packed_xT = pack_weight(n((K, T)) * s)
    packed_eT = pack_weight(n((K, W)) * s)
    return {
        "x_words": packed_xT[0],
        "x_scales": packed_xT[1],
        "e_words": packed_eT[0],
        "e_scales": packed_eT[1],
        "w1": (n((K, N)) / np.sqrt(K) / s).astype(np.float32),
        "w2": (n((K, N)) / np.sqrt(K) / s).astype(np.float32),
        "theta": (n((N, 4))).astype(np.float32),
        "offs": striped(np.random.permutation(T)[:S]),
        "item": striped(np.random.permutation(W)[:S]),
    }


def reference(x_words, x_scales, e_words, e_scales, w1, w2, theta, offs, item):
    xq = unpack_weight(x_words, x_scales)[:, unstriped(offs)]
    a = sigmoid(mxq(f64(w1), 0, "e4m3").T @ xq)
    e_item = unpack_weight(e_words, e_scales)[:, unstriped(item)]
    p = sigmoid(mxq(f64(w2), 0, "e4m3").T @ e_item)
    ap = a * p
    a0 = a - ap
    p0 = p - ap
    c0 = ap - a - p + 1.0
    out_0 = f64(theta)[:, 1:2] * a0 + f64(theta)[:, 2:3] * p0 + f64(theta)[:, 3:4] * ap + f64(theta)[:, 0:1] * c0
    return (out_0,) + planes(out_0)

@@ -1,0 +1,200 @@
+from contextlib import ExitStack
+
+import concourse.mybir as mybir
+
+F32 = mybir.dt.float32
+BF16 = mybir.dt.bfloat16
+I32 = mybir.dt.int32
+U32 = mybir.dt.uint32
+U16 = mybir.dt.uint16
+U8 = mybir.dt.uint8
+FP8X4 = mybir.dt.float8_e4m3fn_x4
+ALU = mybir.AluOpType
+ACT = mybir.ActivationFunctionType
+
+P = 128
+PACK = 4
+K = 512
+M = 512
+S = 512
+HALF = 256
+FLOPS = 2 * 2 * K * M * S
+CHUNKS = ((0, 256), (256, 128), (384, 128))
+
+
+def tile_picked_ylatt_lin_po_kernel(
+    tc, x_words, x_scales, e_words, e_scales, w1, w2, theta, offs, item, out_0, out_1, out_2
+):
+    nc = tc.nc
+    users = x_words.shape[2]
+    items = e_words.shape[2]
+
+    with ExitStack() as ctx:
+        sb = ctx.enter_context(tc.tile_pool(name="sb", bufs=1))
+        ps = ctx.enter_context(tc.psum_pool(name="ps", bufs=1))
+
+        offs_sb = sb.tile([P, S // 16], U16, name="offs_sb")
+        item_sb = sb.tile([P, S // 16], U16, name="item_sb")
+        xw_table = sb.tile([P, users], I32, name="xw_table")
+        ew_table = sb.tile([P, items], I32, name="ew_table", tag="ew_then_u")
+        xs_table = sb.tile([P, users], U8, name="xs_table")
+        es_table = sb.tile([P, items], U8, name="es_table")
+        theta_sb = sb.tile([P, PACK, 4], F32, name="theta_sb")
+        w1_raw = [sb.tile([P, PACK, HALF], F32, name="w1_raw%d" % h) for h in range(2)]
+        w2_raw = [sb.tile([P, PACK, HALF], F32, name="w2_raw%d" % h, tag="w2_raw%d" % h) for h in range(2)]
+
+        def load_scales(queue, table, scales):
+            for q in range(4):
+                queue.dma_start(
+                    out=table[32 * q : 32 * q + 4, :].bitcast(I32),
+                    in_=scales[0, 4 * q : 4 * q + 4, :].bitcast(I32),
+                )
+
+
+        nc.gpsimd.memset(xs_table[:].bitcast(I32), 0)
+        nc.gpsimd.memset(es_table[:].bitcast(I32), 0)
+        warm_in = sb.tile([P, 1], F32, name="warm_in")
+        warm_out = sb.tile([P, 1], F32, name="warm_out")
+        nc.vector.memset(warm_in[:], 0.0)
+        nc.scalar.activation(warm_out[:], warm_in[:], ACT.Sigmoid)
+
+        def load_weight(raw, w, h):
+            rows = w.rearrange("(p j) m -> p j m", j=PACK)
+            nc.sync.dma_start(out=raw[h][:], in_=rows[:, :, h * HALF : (h + 1) * HALF])
+
+        nc.gpsimd.dma_start(out=theta_sb[:], in_=theta.rearrange("(p t) c -> p t c", t=PACK))
+        nc.sync.dma_start(offs_sb[:], offs)
+        load_weight(w1_raw, w1, 0)
+        load_scales(nc.sync, xs_table, x_scales)
+        load_weight(w1_raw, w1, 1)
+        nc.sync.dma_start(out=xw_table[:], in_=x_words[0].rearrange("p c r -> p (c r)").bitcast(I32))
+        nc.sync.dma_start(item_sb[:], item)
+        load_scales(nc.sync, es_table, e_scales)
+        load_weight(w2_raw, w2, 0)
+        load_weight(w2_raw, w2, 1)
+        nc.sync.dma_start(out=ew_table[:], in_=e_words[0].rearrange("p c r -> p (c r)").bitcast(I32))
+
+        c1 = sb.tile([P, PACK], F32, name="c1")
+        c2 = sb.tile([P, PACK], F32, name="c2")
+        c32 = sb.tile([P, PACK], F32, name="c32")
+        c3 = sb.tile([P, PACK], F32, name="c3")
+        nc.gpsimd.tensor_tensor(c1[:], theta_sb[:, :, 1], theta_sb[:, :, 0], ALU.subtract)
+        nc.gpsimd.tensor_tensor(c2[:], theta_sb[:, :, 2], theta_sb[:, :, 0], ALU.subtract)
+        nc.gpsimd.tensor_tensor(c32[:], theta_sb[:, :, 3], theta_sb[:, :, 2], ALU.subtract)
+        nc.gpsimd.tensor_tensor(c3[:], c32[:], c1[:], ALU.subtract)
+
+        grouped = {}
+        codes = {}
+        planes = {}
+        for name in ("w1", "w2"):
+            grouped[name] = sb.tile([P, PACK, P, PACK], BF16, name=name + "_grouped", align_bytes=64)
+            codes[name] = sb.tile([P, M], U32, name=name + "_codes", tag=name + "_codes", align_bytes=64)
+            planes[name] = sb.tile([P, M], U8, name=name + "_plane", align_bytes=64)
+
+        def group_weight(copy, name, raw, m0):
+            cols = raw.shape[2] // PACK
+            copy(
+                out=grouped[name][:, :, m0 : m0 + cols, :].rearrange("p t m j -> p m t j"),
+                in_=raw.rearrange("p j (m t) -> p m t j", t=PACK),
+            )
+
+        def quantize_weight(name, t0, t1):
+            nc.vector.quantize_mx(
+                out=codes[name][:, t0 * P : t1 * P].bitcast(FP8X4),
+                scales=planes[name][:, t0 * P : t1 * P],
+                in_=grouped[name][:, t0:t1, :, :].rearrange("p t m j -> p (t m j)"),
+            )
+
+        def product(acc, name, t, words, plane):
+            nc.tensor.matmul_mx(
+                out=acc,
+                lhsT=codes[name][:, t * P : (t + 1) * P].bitcast(FP8X4),
+                lhsT_scale=planes[name][:, t * P : (t + 1) * P],
+                rhs=words.bitcast(FP8X4),
+                rhs_scale=plane,
+                start=True,
+                stop=True,
+            )
+
+        xw = sb.tile([P, S], U32, name="xw", align_bytes=64)
+        xs = sb.tile([P, S], U8, name="xs", align_bytes=64)
+        es = sb.tile([P, S], U8, name="es", align_bytes=64)
+        nc.vector.tensor_copy(xs[:], xs_table[:].indirect(offs_sb[:]))
+        nc.vector.tensor_copy(xw[:], xw_table[:].bitcast(U32).indirect(offs_sb[:]))
+
+        group_weight(nc.scalar.copy, "w1", w1_raw[0][:], 0)
+        group_weight(nc.scalar.copy, "w1", w1_raw[1][:], HALF // PACK)
+        group_weight(nc.scalar.copy, "w2", w2_raw[0][:], 0)
+        a = sb.tile([P, PACK, S], F32, name="a", tag="w2_raw0")
+        for t in range(PACK):
+            quantize_weight("w1", t, t + 1)
+        for t in range(PACK):
+            acc = ps.tile([P, S], F32, name="acc_a%d" % t)
+            product(acc[:], "w1", t, xw[:], xs[:])
+            nc.scalar.activation(a[:, t, :], acc[:], ACT.Sigmoid)
+
+        nc.vector.tensor_copy(es[:], es_table[:].indirect(item_sb[:]))
+        group_weight(nc.vector.tensor_copy, "w2", w2_raw[1][:], HALF // PACK)
+        quantize_weight("w2", 0, PACK)
+
+        p = sb.tile([P, PACK, S], F32, name="p")
+        for h in range(2):
+            cols = slice(h * HALF, (h + 1) * HALF)
+            ew = sb.tile([P, HALF], U32, name="ew%d" % h, align_bytes=64)
+            nc.vector.tensor_copy(
+                ew[:], ew_table[:].bitcast(U32).indirect(item_sb[:, h * HALF // 16 : (h + 1) * HALF // 16])
+            )
+            for pair in range(2):
+                acc = ps.tile([P, 2, HALF], F32, name="acc_p%d%d" % (h, pair))
+                for i in range(2):
+                    product(acc[:, i, :], "w2", 2 * pair + i, ew[:], es[:, cols])
+                nc.scalar.activation(p[:, 2 * pair : 2 * pair + 2, cols], acc[:], ACT.Sigmoid)
+
+        v = sb.tile([P, PACK, S], F32, name="v", tag="w1_codes", align_bytes=64)
+        for t in range(PACK):
+            nc.scalar.activation(
+                v[:, t, :], a[:, t, :], ACT.Identity, bias=theta_sb[:, t, 0:1], scale=c1[:, t : t + 1]
+            )
+
+        u = [
+            sb.tile([P, 2, S], F32, name="u_low"),
+            sb.tile([P, 2, S], F32, name="u_high", tag="ew_then_u"),
+        ]
+        for t in range(PACK):
+            nc.vector.tensor_scalar(
+                u[t // 2][:, t % 2, :], a[:, t, :], c3[:, t : t + 1], c2[:, t : t + 1], ALU.mult, ALU.add
+            )
+
+        y_rows = out_0.rearrange("(p t) j -> p t j", t=PACK)
+        y_words = out_1[0].rearrange("p c r -> p (c r)").bitcast(I32)
+        y_codes = sb.tile([P, S], U32, name="y_codes", align_bytes=64)
+        y_plane = sb.tile([P, S], U8, name="y_plane", align_bytes=64)
+        for n, (j0, width) in enumerate(CHUNKS):
+            cols = slice(j0, j0 + width)
+            last = n == len(CHUNKS) - 1
+            up = sb.tile([P, PACK, width], F32, name="up%d" % n)
+            y = sb.tile([P, PACK, width], F32, name="y%d" % n)
+            y_grouped = sb.tile([P, width, PACK], BF16, name="y_grouped%d" % n, align_bytes=64)
+            pairs = [slice(0, 2), slice(2, 4)]
+            for pair, ts in enumerate(pairs):
+                nc.vector.tensor_tensor(up[:, ts, :], u[pair][:, :, cols], p[:, ts, cols], ALU.mult)
+            for ts in pairs if n == 0 else [slice(0, PACK)]:
+                nc.vector.tensor_tensor(y[:, ts, :], up[:, ts, :], v[:, ts, cols], ALU.add)
+                nc.sync.dma_start(out=y_rows[:, ts, cols], in_=y[:, ts, :])
+            copy = nc.vector.tensor_copy if last else nc.scalar.copy
+            copy(
+                out=y_grouped[:].rearrange("p (c i) t -> p c t i", i=4),
+                in_=y[:].rearrange("p t (c i) -> p c t i", i=4),
+            )
+            nc.vector.quantize_mx(
+                out=y_codes[:, cols].bitcast(FP8X4),
+                scales=y_plane[:, cols],
+                in_=y_grouped[:].rearrange("p c t -> p (c t)"),
+            )
+            nc.sync.dma_start(out=y_words[:, cols], in_=y_codes[:, cols].bitcast(I32))
+        for q in range(4):
+            queue = nc.scalar if q % 2 else nc.sync
+            queue.dma_start(
+                out=out_2[0, 4 * q : 4 * q + 4, :].bitcast(I32),
+                in_=y_plane[32 * q : 32 * q + 4, :].bitcast(I32),
+            )

@@ -44,10 +44,10 @@ def tile_picked_ylatt_lin_po_kernel(
         w2_raw = [sb.tile([P, PACK, HALF], F32, name="w2_raw%d" % h, tag="w2_raw%d" % h) for h in range(2)]
 
         def load_scales(queue, table, scales):
-            for q in range(4):
+            for r in range(4):
                 queue.dma_start(
-                    out=table[32 * q : 32 * q + 4, :].bitcast(I32),
-                    in_=scales[0, 4 * q : 4 * q + 4, :].bitcast(I32),
+                    out=table[r:P:32, :].bitcast(I32),
+                    in_=scales[0, r:16:4, :].bitcast(I32),
                 )
 
 
@@ -150,48 +150,76 @@ def tile_picked_ylatt_lin_po_kernel(
                     product(acc[:, i, :], "w2", 2 * pair + i, ew[:], es[:, cols])
                 nc.scalar.activation(p[:, 2 * pair : 2 * pair + 2, cols], acc[:], ACT.Sigmoid)
 
-        v = sb.tile([P, PACK, S], F32, name="v", tag="w1_codes", align_bytes=64)
-        for t in range(PACK):
-            nc.scalar.activation(
-                v[:, t, :], a[:, t, :], ACT.Identity, bias=theta_sb[:, t, 0:1], scale=c1[:, t : t + 1]
-            )
-
-        u = [
-            sb.tile([P, 2, S], F32, name="u_low"),
-            sb.tile([P, 2, S], F32, name="u_high", tag="ew_then_u"),
-        ]
+        v_low = sb.tile([P, 2, S], F32, name="v_low", tag="w1_codes", align_bytes=64)
+        u_low = sb.tile([P, 2, S], F32, name="u_low")
+        uv_high = sb.tile([P, 2, 2, S], F32, name="uv_high", tag="ew_then_u")
+        u = [u_low[:], uv_high[:, 0, :, :]]
+        v = [v_low[:], uv_high[:, 1, :, :]]
         for t in range(PACK):
             nc.vector.tensor_scalar(
                 u[t // 2][:, t % 2, :], a[:, t, :], c3[:, t : t + 1], c2[:, t : t + 1], ALU.mult, ALU.add
+            )
+        for t in range(2):
+            nc.scalar.activation(
+                v[0][:, t, :], a[:, t, :], ACT.Identity, bias=theta_sb[:, t, 0:1], scale=c1[:, t : t + 1]
+            )
+        for t in range(2, PACK):
+            nc.vector.tensor_scalar(
+                v[1][:, t - 2, :], a[:, t, :], c1[:, t : t + 1], theta_sb[:, t, 0:1], ALU.mult, ALU.add
             )
 
         y_rows = out_0.rearrange("(p t) j -> p t j", t=PACK)
         y_words = out_1[0].rearrange("p c r -> p (c r)").bitcast(I32)
         y_codes = sb.tile([P, S], U32, name="y_codes", align_bytes=64)
         y_plane = sb.tile([P, S], U8, name="y_plane", align_bytes=64)
-        for n, (j0, width) in enumerate(CHUNKS):
+        up = sb.tile([P, PACK, S], F32, name="up")
+        y = [sb.tile([P, PACK, width], F32, name="y%d" % n) for n, (j0, width) in enumerate(CHUNKS)]
+        y_grouped = [
+            sb.tile([P, width, PACK], BF16, name="y_grouped%d" % n, align_bytes=64)
+            for n, (j0, width) in enumerate(CHUNKS)
+        ]
+
+        def multiply(h):
+            cols = slice(h * HALF, (h + 1) * HALF)
+            for pair in range(2):
+                ts = slice(2 * pair, 2 * pair + 2)
+                nc.vector.tensor_tensor(up[:, ts, cols], u[pair][:, :, cols], p[:, ts, cols], ALU.mult)
+
+        def add(n):
+            j0, width = CHUNKS[n]
             cols = slice(j0, j0 + width)
-            last = n == len(CHUNKS) - 1
-            up = sb.tile([P, PACK, width], F32, name="up%d" % n)
-            y = sb.tile([P, PACK, width], F32, name="y%d" % n)
-            y_grouped = sb.tile([P, width, PACK], BF16, name="y_grouped%d" % n, align_bytes=64)
-            pairs = [slice(0, 2), slice(2, 4)]
-            for pair, ts in enumerate(pairs):
-                nc.vector.tensor_tensor(up[:, ts, :], u[pair][:, :, cols], p[:, ts, cols], ALU.mult)
-            for ts in pairs if n == 0 else [slice(0, PACK)]:
-                nc.vector.tensor_tensor(y[:, ts, :], up[:, ts, :], v[:, ts, cols], ALU.add)
-                nc.sync.dma_start(out=y_rows[:, ts, cols], in_=y[:, ts, :])
-            copy = nc.vector.tensor_copy if last else nc.scalar.copy
+            for pair in range(2):
+                ts = slice(2 * pair, 2 * pair + 2)
+                nc.vector.tensor_tensor(y[n][:, ts, :], up[:, ts, cols], v[pair][:, :, cols], ALU.add)
+            nc.sync.dma_start(out=y_rows[:, :, cols], in_=y[n][:])
+
+        def group_result(copy, n):
             copy(
-                out=y_grouped[:].rearrange("p (c i) t -> p c t i", i=4),
-                in_=y[:].rearrange("p t (c i) -> p c t i", i=4),
+                out=y_grouped[n][:].rearrange("p (c i) t -> p c t i", i=4),
+                in_=y[n][:].rearrange("p t (c i) -> p c t i", i=4),
             )
+
+        def quantize_result(n):
+            j0, width = CHUNKS[n]
+            cols = slice(j0, j0 + width)
             nc.vector.quantize_mx(
                 out=y_codes[:, cols].bitcast(FP8X4),
                 scales=y_plane[:, cols],
-                in_=y_grouped[:].rearrange("p c t -> p (c t)"),
+                in_=y_grouped[n][:].rearrange("p c t -> p (c t)"),
             )
             nc.sync.dma_start(out=y_words[:, cols], in_=y_codes[:, cols].bitcast(I32))
+
+        multiply(0)
+        add(0)
+        group_result(nc.scalar.copy, 0)
+        multiply(1)
+        add(1)
+        group_result(nc.scalar.copy, 1)
+        add(2)
+        quantize_result(0)
+        group_result(nc.vector.tensor_copy, 2)
+        quantize_result(1)
+        quantize_result(2)
         for q in range(4):
             queue = nc.scalar if q % 2 else nc.sync
             queue.dma_start(

@@ -19,6 +19,7 @@ M = 512
 S = 512
 HALF = 256
 FLOPS = 2 * 2 * K * M * S
+W1_SPLIT = 176
 CHUNKS = ((0, 256), (256, 128), (384, 128))
 
 
@@ -40,8 +41,8 @@ def tile_picked_ylatt_lin_po_kernel(
         xs_table = sb.tile([P, users], U8, name="xs_table")
         es_table = sb.tile([P, items], U8, name="es_table")
         theta_sb = sb.tile([P, PACK, 4], F32, name="theta_sb")
-        w1_raw = [sb.tile([P, PACK, HALF], F32, name="w1_raw%d" % h) for h in range(2)]
-        w2_raw = [sb.tile([P, PACK, HALF], F32, name="w2_raw%d" % h, tag="w2_raw%d" % h) for h in range(2)]
+        w1_raw = sb.tile([P, PACK, M], F32, name="w1_raw")
+        w2_raw = sb.tile([P, PACK, M], F32, name="w2_raw")
 
         def load_scales(queue, table, scales):
             for r in range(4):
@@ -58,20 +59,14 @@ def tile_picked_ylatt_lin_po_kernel(
         nc.vector.memset(warm_in[:], 0.0)
         nc.scalar.activation(warm_out[:], warm_in[:], ACT.Sigmoid)
 
-        def load_weight(raw, w, h):
-            rows = w.rearrange("(p j) m -> p j m", j=PACK)
-            nc.sync.dma_start(out=raw[h][:], in_=rows[:, :, h * HALF : (h + 1) * HALF])
-
         nc.gpsimd.dma_start(out=theta_sb[:], in_=theta.rearrange("(p t) c -> p t c", t=PACK))
         nc.sync.dma_start(offs_sb[:], offs)
-        load_weight(w1_raw, w1, 0)
-        load_scales(nc.sync, xs_table, x_scales)
-        load_weight(w1_raw, w1, 1)
         nc.sync.dma_start(out=xw_table[:], in_=x_words[0].rearrange("p c r -> p (c r)").bitcast(I32))
+        load_scales(nc.sync, xs_table, x_scales)
+        nc.sync.dma_start(out=w1_raw[:], in_=w1.rearrange("(p j) m -> p j m", j=PACK))
         nc.sync.dma_start(item_sb[:], item)
         load_scales(nc.sync, es_table, e_scales)
-        load_weight(w2_raw, w2, 0)
-        load_weight(w2_raw, w2, 1)
+        nc.sync.dma_start(out=w2_raw[:], in_=w2.rearrange("(p j) m -> p j m", j=PACK))
         nc.sync.dma_start(out=ew_table[:], in_=e_words[0].rearrange("p c r -> p (c r)").bitcast(I32))
 
         c1 = sb.tile([P, PACK], F32, name="c1")
@@ -87,7 +82,7 @@ def tile_picked_ylatt_lin_po_kernel(
         codes = {}
         planes = {}
         for name in ("w1", "w2"):
-            grouped[name] = sb.tile([P, PACK, P, PACK], BF16, name=name + "_grouped", align_bytes=64)
+            grouped[name] = sb.tile([P, PACK, P, PACK], BF16, name=name + "_grouped", tag=name + "_grouped", align_bytes=64)
             codes[name] = sb.tile([P, M], U32, name=name + "_codes", tag=name + "_codes", align_bytes=64)
             planes[name] = sb.tile([P, M], U8, name=name + "_plane", align_bytes=64)
 
@@ -119,13 +114,12 @@ def tile_picked_ylatt_lin_po_kernel(
         xw = sb.tile([P, S], U32, name="xw", align_bytes=64)
         xs = sb.tile([P, S], U8, name="xs", align_bytes=64)
         es = sb.tile([P, S], U8, name="es", align_bytes=64)
-        nc.vector.tensor_copy(xs[:], xs_table[:].indirect(offs_sb[:]))
         nc.vector.tensor_copy(xw[:], xw_table[:].bitcast(U32).indirect(offs_sb[:]))
+        nc.vector.tensor_copy(xs[:], xs_table[:].indirect(offs_sb[:]))
 
-        group_weight(nc.scalar.copy, "w1", w1_raw[0][:], 0)
-        group_weight(nc.scalar.copy, "w1", w1_raw[1][:], HALF // PACK)
-        group_weight(nc.scalar.copy, "w2", w2_raw[0][:], 0)
-        a = sb.tile([P, PACK, S], F32, name="a", tag="w2_raw0")
+        group_weight(nc.scalar.copy, "w1", w1_raw[:, :, :W1_SPLIT], 0)
+        group_weight(nc.vector.tensor_copy, "w1", w1_raw[:, :, W1_SPLIT:], W1_SPLIT // PACK)
+        a = sb.tile([P, PACK, S], F32, name="a")
         for t in range(PACK):
             quantize_weight("w1", t, t + 1)
         for t in range(PACK):
@@ -134,38 +128,31 @@ def tile_picked_ylatt_lin_po_kernel(
             nc.scalar.activation(a[:, t, :], acc[:], ACT.Sigmoid)
 
         nc.vector.tensor_copy(es[:], es_table[:].indirect(item_sb[:]))
-        group_weight(nc.vector.tensor_copy, "w2", w2_raw[1][:], HALF // PACK)
+        group_weight(nc.vector.tensor_copy, "w2", w2_raw[:], 0)
         quantize_weight("w2", 0, PACK)
 
         p = sb.tile([P, PACK, S], F32, name="p")
+        ew = sb.tile([P, S], U32, name="ew", tag="w2_grouped", align_bytes=64)
         for h in range(2):
             cols = slice(h * HALF, (h + 1) * HALF)
-            ew = sb.tile([P, HALF], U32, name="ew%d" % h, align_bytes=64)
             nc.vector.tensor_copy(
-                ew[:], ew_table[:].bitcast(U32).indirect(item_sb[:, h * HALF // 16 : (h + 1) * HALF // 16])
+                ew[:, cols], ew_table[:].bitcast(U32).indirect(item_sb[:, h * HALF // 16 : (h + 1) * HALF // 16])
             )
             for pair in range(2):
                 acc = ps.tile([P, 2, HALF], F32, name="acc_p%d%d" % (h, pair))
                 for i in range(2):
-                    product(acc[:, i, :], "w2", 2 * pair + i, ew[:], es[:, cols])
+                    product(acc[:, i, :], "w2", 2 * pair + i, ew[:, cols], es[:, cols])
                 nc.scalar.activation(p[:, 2 * pair : 2 * pair + 2, cols], acc[:], ACT.Sigmoid)
 
+        u = sb.tile([P, PACK, S], F32, name="u", tag="ew_then_u")
         v_low = sb.tile([P, 2, S], F32, name="v_low", tag="w1_codes", align_bytes=64)
-        u_low = sb.tile([P, 2, S], F32, name="u_low")
-        uv_high = sb.tile([P, 2, 2, S], F32, name="uv_high", tag="ew_then_u")
-        u = [u_low[:], uv_high[:, 0, :, :]]
-        v = [v_low[:], uv_high[:, 1, :, :]]
+        v_high = sb.tile([P, 2, S], F32, name="v_high", tag="w2_grouped", align_bytes=64)
+        v = [v_low[:], v_high[:]]
         for t in range(PACK):
-            nc.vector.tensor_scalar(
-                u[t // 2][:, t % 2, :], a[:, t, :], c3[:, t : t + 1], c2[:, t : t + 1], ALU.mult, ALU.add
-            )
-        for t in range(2):
+            nc.vector.tensor_scalar(u[:, t, :], a[:, t, :], c3[:, t : t + 1], c2[:, t : t + 1], ALU.mult, ALU.add)
+        for t in range(PACK):
             nc.scalar.activation(
-                v[0][:, t, :], a[:, t, :], ACT.Identity, bias=theta_sb[:, t, 0:1], scale=c1[:, t : t + 1]
-            )
-        for t in range(2, PACK):
-            nc.vector.tensor_scalar(
-                v[1][:, t - 2, :], a[:, t, :], c1[:, t : t + 1], theta_sb[:, t, 0:1], ALU.mult, ALU.add
+                v[t // 2][:, t % 2, :], a[:, t, :], ACT.Identity, bias=theta_sb[:, t, 0:1], scale=c1[:, t : t + 1]
             )
 
         y_rows = out_0.rearrange("(p t) j -> p t j", t=PACK)
@@ -173,7 +160,7 @@ def tile_picked_ylatt_lin_po_kernel(
         y_codes = sb.tile([P, S], U32, name="y_codes", align_bytes=64)
         y_plane = sb.tile([P, S], U8, name="y_plane", align_bytes=64)
         up = sb.tile([P, PACK, S], F32, name="up")
-        y = [sb.tile([P, PACK, width], F32, name="y%d" % n) for n, (j0, width) in enumerate(CHUNKS)]
+        y = sb.tile([P, PACK, S], F32, name="y")
         y_grouped = [
             sb.tile([P, width, PACK], BF16, name="y_grouped%d" % n, align_bytes=64)
             for n, (j0, width) in enumerate(CHUNKS)
@@ -183,20 +170,19 @@ def tile_picked_ylatt_lin_po_kernel(
             cols = slice(h * HALF, (h + 1) * HALF)
             for pair in range(2):
                 ts = slice(2 * pair, 2 * pair + 2)
-                nc.vector.tensor_tensor(up[:, ts, cols], u[pair][:, :, cols], p[:, ts, cols], ALU.mult)
+                nc.vector.tensor_tensor(up[:, ts, cols], u[:, ts, cols], p[:, ts, cols], ALU.mult)
 
-        def add(n):
-            j0, width = CHUNKS[n]
+        def add(pair, j0, width):
             cols = slice(j0, j0 + width)
-            for pair in range(2):
-                ts = slice(2 * pair, 2 * pair + 2)
-                nc.vector.tensor_tensor(y[n][:, ts, :], up[:, ts, cols], v[pair][:, :, cols], ALU.add)
-            nc.sync.dma_start(out=y_rows[:, :, cols], in_=y[n][:])
+            ts = slice(2 * pair, 2 * pair + 2)
+            nc.vector.tensor_tensor(y[:, ts, cols], up[:, ts, cols], v[pair][:, :, cols], ALU.add)
+            nc.sync.dma_start(out=y_rows[:, ts, cols], in_=y[:, ts, cols])
 
         def group_result(copy, n):
+            j0, width = CHUNKS[n]
             copy(
                 out=y_grouped[n][:].rearrange("p (c i) t -> p c t i", i=4),
-                in_=y[n][:].rearrange("p t (c i) -> p c t i", i=4),
+                in_=y[:, :, j0 : j0 + width].rearrange("p t (c i) -> p c t i", i=4),
             )
 
         def quantize_result(n):
@@ -210,12 +196,14 @@ def tile_picked_ylatt_lin_po_kernel(
             nc.sync.dma_start(out=y_words[:, cols], in_=y_codes[:, cols].bitcast(I32))
 
         multiply(0)
-        add(0)
-        group_result(nc.scalar.copy, 0)
+        add(0, 0, HALF)
         multiply(1)
-        add(1)
+        add(1, 0, HALF)
+        group_result(nc.scalar.copy, 0)
+        add(0, HALF, HALF)
+        add(1, *CHUNKS[1])
         group_result(nc.scalar.copy, 1)
-        add(2)
+        add(1, *CHUNKS[2])
         quantize_result(0)
         group_result(nc.vector.tensor_copy, 2)
         quantize_result(1)

@@ -12,14 +12,15 @@ FP8X4 = mybir.dt.float8_e4m3fn_x4
 ALU = mybir.AluOpType
 ACT = mybir.ActivationFunctionType
 
-P = 128
+PARTS = 128
 PACK = 4
 K = 512
 M = 512
 S = 512
 HALF = 256
+PER_COLUMN = 16
 FLOPS = 2 * 2 * K * M * S
-W1_SPLIT = 176
+
 CHUNKS = ((0, 256), (256, 128), (384, 128))
 
 
@@ -34,180 +35,200 @@ def tile_picked_ylatt_lin_po_kernel(
         sb = ctx.enter_context(tc.tile_pool(name="sb", bufs=1))
         ps = ctx.enter_context(tc.psum_pool(name="ps", bufs=1))
 
-        offs_sb = sb.tile([P, S // 16], U16, name="offs_sb")
-        item_sb = sb.tile([P, S // 16], U16, name="item_sb")
-        xw_table = sb.tile([P, users], I32, name="xw_table")
-        ew_table = sb.tile([P, items], I32, name="ew_table", tag="ew_then_u")
-        xs_table = sb.tile([P, users], U8, name="xs_table")
-        es_table = sb.tile([P, items], U8, name="es_table")
-        theta_sb = sb.tile([P, PACK, 4], F32, name="theta_sb")
-        w1_raw = sb.tile([P, PACK, M], F32, name="w1_raw")
-        w2_raw = sb.tile([P, PACK, M], F32, name="w2_raw")
+        offs_sb = sb.tile([PARTS, S // PER_COLUMN], U16, name="offs_sb")
+        item_sb = sb.tile([PARTS, S // PER_COLUMN], U16, name="item_sb")
+        x_word_table = sb.tile([PARTS, users], I32, name="x_word_table")
+        e_word_table = sb.tile([PARTS, items], I32, name="e_word_table", tag="e_word_table")
+        x_scale_table = sb.tile([PARTS, users], U8, name="x_scale_table")
+        e_scale_table = sb.tile([PARTS, items], U8, name="e_scale_table")
+        theta_sb = sb.tile([PARTS, PACK, 4], F32, name="theta_sb")
+        w1_raw = [sb.tile([PARTS, PACK, HALF], F32, name="w1_raw%d" % h) for h in range(2)]
+        w2_raw = sb.tile([PARTS, PACK, M], F32, name="w2_raw")
 
-        def load_scales(queue, table, scales):
+        def load_words(table, words):
+            nc.sync.dma_start(out=table[:], in_=words[0].rearrange("p c r -> p (c r)").bitcast(I32))
+
+        def load_scales(table, scales):
             for r in range(4):
-                queue.dma_start(
-                    out=table[r:P:32, :].bitcast(I32),
+                nc.sync.dma_start(
+                    out=table[r:PARTS:32, :].bitcast(I32),
                     in_=scales[0, r:16:4, :].bitcast(I32),
                 )
 
-
-        nc.gpsimd.memset(xs_table[:].bitcast(I32), 0)
-        nc.gpsimd.memset(es_table[:].bitcast(I32), 0)
-        warm_in = sb.tile([P, 1], F32, name="warm_in")
-        warm_out = sb.tile([P, 1], F32, name="warm_out")
-        nc.vector.memset(warm_in[:], 0.0)
-        nc.scalar.activation(warm_out[:], warm_in[:], ACT.Sigmoid)
+        nc.gpsimd.memset(x_scale_table[:].bitcast(I32), 0)
+        nc.gpsimd.memset(e_scale_table[:].bitcast(I32), 0)
 
         nc.gpsimd.dma_start(out=theta_sb[:], in_=theta.rearrange("(p t) c -> p t c", t=PACK))
         nc.sync.dma_start(offs_sb[:], offs)
-        nc.sync.dma_start(out=xw_table[:], in_=x_words[0].rearrange("p c r -> p (c r)").bitcast(I32))
-        load_scales(nc.sync, xs_table, x_scales)
-        nc.sync.dma_start(out=w1_raw[:], in_=w1.rearrange("(p j) m -> p j m", j=PACK))
+        load_words(x_word_table, x_words)
+        load_scales(x_scale_table, x_scales)
+        w1_rows = w1.rearrange("(p j) m -> p j m", j=PACK)
+        for h in range(2):
+            nc.sync.dma_start(out=w1_raw[h][:], in_=w1_rows[:, :, h * HALF : (h + 1) * HALF])
         nc.sync.dma_start(item_sb[:], item)
-        load_scales(nc.sync, es_table, e_scales)
+        load_scales(e_scale_table, e_scales)
         nc.sync.dma_start(out=w2_raw[:], in_=w2.rearrange("(p j) m -> p j m", j=PACK))
-        nc.sync.dma_start(out=ew_table[:], in_=e_words[0].rearrange("p c r -> p (c r)").bitcast(I32))
+        load_words(e_word_table, e_words)
 
-        c1 = sb.tile([P, PACK], F32, name="c1")
-        c2 = sb.tile([P, PACK], F32, name="c2")
-        c32 = sb.tile([P, PACK], F32, name="c32")
-        c3 = sb.tile([P, PACK], F32, name="c3")
-        nc.gpsimd.tensor_tensor(c1[:], theta_sb[:, :, 1], theta_sb[:, :, 0], ALU.subtract)
-        nc.gpsimd.tensor_tensor(c2[:], theta_sb[:, :, 2], theta_sb[:, :, 0], ALU.subtract)
-        nc.gpsimd.tensor_tensor(c32[:], theta_sb[:, :, 3], theta_sb[:, :, 2], ALU.subtract)
-        nc.gpsimd.tensor_tensor(c3[:], c32[:], c1[:], ALU.subtract)
+        c0 = theta_sb[:, :, 0]
+        c1 = sb.tile([PARTS, PACK], F32, name="c1")
+        c2 = sb.tile([PARTS, PACK], F32, name="c2")
+        theta3_less_theta2 = sb.tile([PARTS, PACK], F32, name="theta3_less_theta2")
+        c3 = sb.tile([PARTS, PACK], F32, name="c3")
+        nc.gpsimd.tensor_tensor(c1[:], theta_sb[:, :, 1], c0, ALU.subtract)
+        nc.gpsimd.tensor_tensor(c2[:], theta_sb[:, :, 2], c0, ALU.subtract)
+        nc.gpsimd.tensor_tensor(theta3_less_theta2[:], theta_sb[:, :, 3], theta_sb[:, :, 2], ALU.subtract)
+        nc.gpsimd.tensor_tensor(c3[:], theta3_less_theta2[:], c1[:], ALU.subtract)
 
-        grouped = {}
+        dealt = {}
         codes = {}
         planes = {}
-        for name in ("w1", "w2"):
-            grouped[name] = sb.tile([P, PACK, P, PACK], BF16, name=name + "_grouped", tag=name + "_grouped", align_bytes=64)
-            codes[name] = sb.tile([P, M], U32, name=name + "_codes", tag=name + "_codes", align_bytes=64)
-            planes[name] = sb.tile([P, M], U8, name=name + "_plane", align_bytes=64)
+        for w in ("w1", "w2"):
+            dealt[w] = sb.tile([PARTS, PACK, PARTS, PACK], BF16, name=w + "_dealt", tag=w + "_dealt", align_bytes=64)
+            codes[w] = sb.tile([PARTS, M], U32, name=w + "_codes", tag=w + "_codes", align_bytes=64)
+            planes[w] = sb.tile([PARTS, M], U8, name=w + "_plane", align_bytes=64)
 
-        def group_weight(copy, name, raw, m0):
-            cols = raw.shape[2] // PACK
+        def deal_weight(copy, w, raw, first_column):
+            m0 = first_column // PACK
             copy(
-                out=grouped[name][:, :, m0 : m0 + cols, :].rearrange("p t m j -> p m t j"),
+                out=dealt[w][:, :, m0 : m0 + raw.shape[2] // PACK, :].rearrange("p t m j -> p m t j"),
                 in_=raw.rearrange("p j (m t) -> p m t j", t=PACK),
             )
 
-        def quantize_weight(name, t0, t1):
+        def quantize_weight(w, t0, t1):
             nc.vector.quantize_mx(
-                out=codes[name][:, t0 * P : t1 * P].bitcast(FP8X4),
-                scales=planes[name][:, t0 * P : t1 * P],
-                in_=grouped[name][:, t0:t1, :, :].rearrange("p t m j -> p (t m j)"),
+                out=codes[w][:, t0 * PARTS : t1 * PARTS].bitcast(FP8X4),
+                scales=planes[w][:, t0 * PARTS : t1 * PARTS],
+                in_=dealt[w][:, t0:t1, :, :].rearrange("p t m j -> p (t m j)"),
             )
 
-        def product(acc, name, t, words, plane):
+        def product(acc, w, t, words, plane):
             nc.tensor.matmul_mx(
                 out=acc,
-                lhsT=codes[name][:, t * P : (t + 1) * P].bitcast(FP8X4),
-                lhsT_scale=planes[name][:, t * P : (t + 1) * P],
+                lhsT=codes[w][:, t * PARTS : (t + 1) * PARTS].bitcast(FP8X4),
+                lhsT_scale=planes[w][:, t * PARTS : (t + 1) * PARTS],
                 rhs=words.bitcast(FP8X4),
                 rhs_scale=plane,
                 start=True,
                 stop=True,
             )
 
-        xw = sb.tile([P, S], U32, name="xw", align_bytes=64)
-        xs = sb.tile([P, S], U8, name="xs", align_bytes=64)
-        es = sb.tile([P, S], U8, name="es", align_bytes=64)
-        nc.vector.tensor_copy(xw[:], xw_table[:].bitcast(U32).indirect(offs_sb[:]))
-        nc.vector.tensor_copy(xs[:], xs_table[:].indirect(offs_sb[:]))
-
-        group_weight(nc.scalar.copy, "w1", w1_raw[:, :, :W1_SPLIT], 0)
-        group_weight(nc.vector.tensor_copy, "w1", w1_raw[:, :, W1_SPLIT:], W1_SPLIT // PACK)
-        a = sb.tile([P, PACK, S], F32, name="a")
+        x_picked = sb.tile([PARTS, S], U32, name="x_picked", align_bytes=64)
+        x_plane = sb.tile([PARTS, S], U8, name="x_plane", align_bytes=64)
+        nc.vector.tensor_copy(x_picked[:], x_word_table[:].bitcast(U32).indirect(offs_sb[:]))
+        nc.vector.tensor_copy(x_plane[:], x_scale_table[:].indirect(offs_sb[:]))
+        deal_weight(nc.scalar.copy, "w1", w1_raw[0][:], 0)
+        deal_weight(nc.vector.tensor_copy, "w1", w1_raw[1][:], HALF)
         for t in range(PACK):
             quantize_weight("w1", t, t + 1)
+        a = sb.tile([PARTS, PACK, S], F32, name="a")
         for t in range(PACK):
-            acc = ps.tile([P, S], F32, name="acc_a%d" % t)
-            product(acc[:], "w1", t, xw[:], xs[:])
-            nc.scalar.activation(a[:, t, :], acc[:], ACT.Sigmoid)
+            acc_a = ps.tile([PARTS, S], F32, name="acc_a%d" % t)
+            product(acc_a[:], "w1", t, x_picked[:], x_plane[:])
+            nc.scalar.activation(a[:, t, :], acc_a[:], ACT.Sigmoid)
 
-        nc.vector.tensor_copy(es[:], es_table[:].indirect(item_sb[:]))
-        group_weight(nc.vector.tensor_copy, "w2", w2_raw[:], 0)
+        e_plane = sb.tile([PARTS, S], U8, name="e_plane", align_bytes=64)
+        nc.vector.tensor_copy(e_plane[:], e_scale_table[:].indirect(item_sb[:]))
+        deal_weight(nc.vector.tensor_copy, "w2", w2_raw[:], 0)
         quantize_weight("w2", 0, PACK)
-
-        p = sb.tile([P, PACK, S], F32, name="p")
-        ew = sb.tile([P, S], U32, name="ew", tag="w2_grouped", align_bytes=64)
+        e_picked = [sb.tile([PARTS, HALF], U32, name="e_picked%d" % h, align_bytes=64) for h in range(2)]
         for h in range(2):
+            offsets = item_sb[:, h * HALF // PER_COLUMN : (h + 1) * HALF // PER_COLUMN]
+            nc.vector.tensor_copy(e_picked[h][:], e_word_table[:].bitcast(U32).indirect(offsets))
+        p = sb.tile([PARTS, PACK, S], F32, name="p")
+
+        def item_coordinate(h):
             cols = slice(h * HALF, (h + 1) * HALF)
-            nc.vector.tensor_copy(
-                ew[:, cols], ew_table[:].bitcast(U32).indirect(item_sb[:, h * HALF // 16 : (h + 1) * HALF // 16])
-            )
             for pair in range(2):
-                acc = ps.tile([P, 2, HALF], F32, name="acc_p%d%d" % (h, pair))
+                acc_p = ps.tile([PARTS, 2, HALF], F32, name="acc_p%d%d" % (h, pair))
                 for i in range(2):
-                    product(acc[:, i, :], "w2", 2 * pair + i, ew[:, cols], es[:, cols])
-                nc.scalar.activation(p[:, 2 * pair : 2 * pair + 2, cols], acc[:], ACT.Sigmoid)
+                    product(acc_p[:, i, :], "w2", 2 * pair + i, e_picked[h][:], e_plane[:, cols])
+                nc.scalar.activation(p[:, 2 * pair : 2 * pair + 2, cols], acc_p[:], ACT.Sigmoid)
 
-        u = sb.tile([P, PACK, S], F32, name="u", tag="ew_then_u")
-        v_low = sb.tile([P, 2, S], F32, name="v_low", tag="w1_codes", align_bytes=64)
-        v_high = sb.tile([P, 2, S], F32, name="v_high", tag="w2_grouped", align_bytes=64)
-        v = [v_low[:], v_high[:]]
-        for t in range(PACK):
-            nc.vector.tensor_scalar(u[:, t, :], a[:, t, :], c3[:, t : t + 1], c2[:, t : t + 1], ALU.mult, ALU.add)
-        for t in range(PACK):
-            nc.scalar.activation(
-                v[t // 2][:, t % 2, :], a[:, t, :], ACT.Identity, bias=theta_sb[:, t, 0:1], scale=c1[:, t : t + 1]
-            )
+        item_coordinate(0)
 
-        y_rows = out_0.rearrange("(p t) j -> p t j", t=PACK)
+        uv_first = sb.tile([PARTS, 2, 2, S], F32, name="uv_first", tag="w1_codes", align_bytes=64)
+        u_second = sb.tile([PARTS, 2, S], F32, name="u_second", tag="w2_dealt", align_bytes=64)
+        v_second = sb.tile([PARTS, 2, S], F32, name="v_second", tag="e_word_table")
+        u = [uv_first[:, 0, :, :], u_second[:]]
+        v = [uv_first[:, 1, :, :], v_second[:]]
+        for out, factor, offset in ((u[0], c3, c2), (v[0], c1, c0)):
+            for t in range(2):
+                nc.scalar.activation(
+                    out[:, t, :], a[:, t, :], ACT.Identity, bias=offset[:, t : t + 1], scale=factor[:, t : t + 1]
+                )
+        for engine, out, factor, offset in ((nc.gpsimd, u[1], c3, c2), (nc.vector, v[1], c1, c0)):
+            for t in range(2, PACK):
+                engine.tensor_scalar(
+                    out[:, t - 2, :], a[:, t, :], factor[:, t : t + 1], offset[:, t : t + 1], ALU.mult, ALU.add
+                )
+
+        item_coordinate(1)
+
+        y_rows = out_0.rearrange("(p t) s -> p t s", t=PACK)
         y_words = out_1[0].rearrange("p c r -> p (c r)").bitcast(I32)
-        y_codes = sb.tile([P, S], U32, name="y_codes", align_bytes=64)
-        y_plane = sb.tile([P, S], U8, name="y_plane", align_bytes=64)
-        up = sb.tile([P, PACK, S], F32, name="up")
-        y = sb.tile([P, PACK, S], F32, name="y")
+        up = sb.tile([PARTS, PACK, S], F32, name="up")
+        y = sb.tile([PARTS, PACK, S], F32, name="y")
         y_grouped = [
-            sb.tile([P, width, PACK], BF16, name="y_grouped%d" % n, align_bytes=64)
-            for n, (j0, width) in enumerate(CHUNKS)
+            sb.tile([PARTS, width, PACK], BF16, name="y_grouped%d" % n, align_bytes=64)
+            for n, (first, width) in enumerate(CHUNKS)
         ]
+        y_codes = sb.tile([PARTS, S], U32, name="y_codes", align_bytes=64)
+        y_plane = sb.tile([PARTS, S], U8, name="y_plane", align_bytes=64)
+        pairs = [slice(0, 2), slice(2, 4)]
+        halves = [slice(0, HALF), slice(HALF, S)]
+        chunks = [slice(first, first + width) for first, width in CHUNKS]
 
-        def multiply(h):
-            cols = slice(h * HALF, (h + 1) * HALF)
-            for pair in range(2):
-                ts = slice(2 * pair, 2 * pair + 2)
-                nc.vector.tensor_tensor(up[:, ts, cols], u[:, ts, cols], p[:, ts, cols], ALU.mult)
+        def multiply(pair, cols):
+            ts = pairs[pair]
+            nc.vector.tensor_tensor(up[:, ts, cols], u[pair][:, :, cols], p[:, ts, cols], ALU.mult)
 
-        def add(pair, j0, width):
-            cols = slice(j0, j0 + width)
-            ts = slice(2 * pair, 2 * pair + 2)
+        def add(pair, cols):
+            ts = pairs[pair]
             nc.vector.tensor_tensor(y[:, ts, cols], up[:, ts, cols], v[pair][:, :, cols], ALU.add)
+
+        def store_rows(ts, cols):
             nc.sync.dma_start(out=y_rows[:, ts, cols], in_=y[:, ts, cols])
 
         def group_result(copy, n):
-            j0, width = CHUNKS[n]
             copy(
                 out=y_grouped[n][:].rearrange("p (c i) t -> p c t i", i=4),
-                in_=y[:, :, j0 : j0 + width].rearrange("p t (c i) -> p c t i", i=4),
+                in_=y[:, :, chunks[n]].rearrange("p t (c i) -> p c t i", i=4),
             )
 
         def quantize_result(n):
-            j0, width = CHUNKS[n]
-            cols = slice(j0, j0 + width)
             nc.vector.quantize_mx(
-                out=y_codes[:, cols].bitcast(FP8X4),
-                scales=y_plane[:, cols],
+                out=y_codes[:, chunks[n]].bitcast(FP8X4),
+                scales=y_plane[:, chunks[n]],
                 in_=y_grouped[n][:].rearrange("p c t -> p (c t)"),
             )
+
+        def store_words(cols):
             nc.sync.dma_start(out=y_words[:, cols], in_=y_codes[:, cols].bitcast(I32))
 
-        multiply(0)
-        add(0, 0, HALF)
-        multiply(1)
-        add(1, 0, HALF)
+        for pair in range(2):
+            multiply(pair, halves[0])
+        for pair in range(2):
+            add(pair, halves[0])
+        store_rows(slice(0, PACK), halves[0])
         group_result(nc.scalar.copy, 0)
-        add(0, HALF, HALF)
-        add(1, *CHUNKS[1])
+
+        for pair in range(2):
+            multiply(pair, halves[1])
+        add(0, halves[1])
+        store_rows(pairs[0], halves[1])
+        add(1, chunks[1])
         group_result(nc.scalar.copy, 1)
-        add(1, *CHUNKS[2])
+        add(1, chunks[2])
+        store_rows(pairs[1], halves[1])
+
         quantize_result(0)
+        store_words(halves[0])
         group_result(nc.vector.tensor_copy, 2)
         quantize_result(1)
         quantize_result(2)
+        store_words(halves[1])
+
         for q in range(4):
             queue = nc.scalar if q % 2 else nc.sync
             queue.dma_start(

@@ -21,6 +21,8 @@ HALF = 256
 PER_COLUMN = 16
 FLOPS = 2 * 2 * K * M * S
 
+SCALAR_SHARE = 80
+
 CHUNKS = ((0, 256), (256, 128), (384, 128))
 
 
@@ -57,6 +59,11 @@ def tile_picked_ylatt_lin_po_kernel(
 
         nc.gpsimd.memset(x_scale_table[:].bitcast(I32), 0)
         nc.gpsimd.memset(e_scale_table[:].bitcast(I32), 0)
+
+        warm_in = sb.tile([PARTS, 1], F32, name="warm_in")
+        warm_out = sb.tile([PARTS, 1], F32, name="warm_out")
+        nc.vector.memset(warm_in[:], 0.0)
+        nc.scalar.activation(warm_out[:], warm_in[:], ACT.Sigmoid)
 
         nc.gpsimd.dma_start(out=theta_sb[:], in_=theta.rearrange("(p t) c -> p t c", t=PACK))
         nc.sync.dma_start(offs_sb[:], offs)
@@ -118,7 +125,8 @@ def tile_picked_ylatt_lin_po_kernel(
         nc.vector.tensor_copy(x_picked[:], x_word_table[:].bitcast(U32).indirect(offs_sb[:]))
         nc.vector.tensor_copy(x_plane[:], x_scale_table[:].indirect(offs_sb[:]))
         deal_weight(nc.scalar.copy, "w1", w1_raw[0][:], 0)
-        deal_weight(nc.vector.tensor_copy, "w1", w1_raw[1][:], HALF)
+        deal_weight(nc.scalar.copy, "w1", w1_raw[1][:, :, :SCALAR_SHARE], HALF)
+        deal_weight(nc.vector.tensor_copy, "w1", w1_raw[1][:, :, SCALAR_SHARE:], HALF + SCALAR_SHARE)
         for t in range(PACK):
             quantize_weight("w1", t, t + 1)
         a = sb.tile([PARTS, PACK, S], F32, name="a")

@@ -98,8 +98,8 @@ def tile_picked_ylatt_lin_po_kernel(
         def deal_weight(copy, w, raw, first_column):
             m0 = first_column // PACK
             copy(
-                out=dealt[w][:, :, m0 : m0 + raw.shape[2] // PACK, :].rearrange("p t m j -> p m t j"),
-                in_=raw.rearrange("p j (m t) -> p m t j", t=PACK),
+                out=dealt[w][:, :, m0 : m0 + raw.shape[2] // PACK, :].rearrange("p t m j -> p m j t"),
+                in_=raw.rearrange("p j (m t) -> p m j t", t=PACK),
             )
 
         def quantize_weight(w, t0, t1):

@@ -50,10 +50,10 @@ def tile_picked_ylatt_lin_po_kernel(
         def load_words(table, words):
             nc.sync.dma_start(out=table[:], in_=words[0].rearrange("p c r -> p (c r)").bitcast(I32))
 
-        def load_scales(table, scales):
+        def load_scales(table, scales, first):
             for r in range(4):
                 nc.sync.dma_start(
-                    out=table[r:PARTS:32, :].bitcast(I32),
+                    out=table[first + r : PARTS : 32, :].bitcast(I32),
                     in_=scales[0, r:16:4, :].bitcast(I32),
                 )
 
@@ -66,14 +66,14 @@ def tile_picked_ylatt_lin_po_kernel(
         nc.scalar.activation(warm_out[:], warm_in[:], ACT.Sigmoid)
 
         nc.gpsimd.dma_start(out=theta_sb[:], in_=theta.rearrange("(p t) c -> p t c", t=PACK))
-        nc.sync.dma_start(offs_sb[:], offs)
         load_words(x_word_table, x_words)
-        load_scales(x_scale_table, x_scales)
+        nc.sync.dma_start(offs_sb[:], offs)
+        load_scales(x_scale_table, x_scales, 0)
         w1_rows = w1.rearrange("(p j) m -> p j m", j=PACK)
         for h in range(2):
             nc.sync.dma_start(out=w1_raw[h][:], in_=w1_rows[:, :, h * HALF : (h + 1) * HALF])
         nc.sync.dma_start(item_sb[:], item)
-        load_scales(e_scale_table, e_scales)
+        load_scales(e_scale_table, e_scales, 4)
         nc.sync.dma_start(out=w2_raw[:], in_=w2.rearrange("(p j) m -> p j m", j=PACK))
         load_words(e_word_table, e_words)
 
@@ -131,7 +131,7 @@ def tile_picked_ylatt_lin_po_kernel(
             quantize_weight("w1", t, t + 1)
         a = sb.tile([PARTS, PACK, S], F32, name="a")
         for t in range(PACK):
-            acc_a = ps.tile([PARTS, S], F32, name="acc_a%d" % t)
+            acc_a = ps.tile([PARTS, S], F32, name="acc_a%d" % t, tag="bank%d" % t)
             product(acc_a[:], "w1", t, x_picked[:], x_plane[:])
             nc.scalar.activation(a[:, t, :], acc_a[:], ACT.Sigmoid)
 
@@ -139,39 +139,52 @@ def tile_picked_ylatt_lin_po_kernel(
         nc.vector.tensor_copy(e_plane[:], e_scale_table[:].indirect(item_sb[:]))
         deal_weight(nc.vector.tensor_copy, "w2", w2_raw[:], 0)
         quantize_weight("w2", 0, PACK)
-        e_picked = [sb.tile([PARTS, HALF], U32, name="e_picked%d" % h, align_bytes=64) for h in range(2)]
+        e_picked = [
+            sb.tile([PARTS, HALF], U32, name="e_picked%d" % h, tag="e_picked%d" % h, align_bytes=64) for h in range(2)
+        ]
         for h in range(2):
             offsets = item_sb[:, h * HALF // PER_COLUMN : (h + 1) * HALF // PER_COLUMN]
             nc.vector.tensor_copy(e_picked[h][:], e_word_table[:].bitcast(U32).indirect(offsets))
         p = sb.tile([PARTS, PACK, S], F32, name="p")
 
-        def item_coordinate(h):
-            cols = slice(h * HALF, (h + 1) * HALF)
-            for pair in range(2):
-                acc_p = ps.tile([PARTS, 2, HALF], F32, name="acc_p%d%d" % (h, pair))
-                for i in range(2):
-                    product(acc_p[:, i, :], "w2", 2 * pair + i, e_picked[h][:], e_plane[:, cols])
-                nc.scalar.activation(p[:, 2 * pair : 2 * pair + 2, cols], acc_p[:], ACT.Sigmoid)
+        halves = [slice(0, HALF), slice(HALF, S)]
 
-        item_coordinate(0)
+        def item_coordinate(h, groups, banks):
+            for (t0, t1), bank in zip(groups, banks):
+                acc_p = ps.tile([PARTS, t1 - t0, HALF], F32, name="acc_p%d%d" % (h, t0), tag="bank%d" % bank)
+                for t in range(t0, t1):
+                    product(acc_p[:, t - t0, :], "w2", t, e_picked[h][:], e_plane[4:, halves[h]])
+                nc.scalar.activation(p[:, t0:t1, halves[h]], acc_p[:], ACT.Sigmoid)
+
+        def affine_on_scalar(out, t, cols, factor, offset):
+            nc.scalar.activation(
+                out, a[:, t, cols], ACT.Identity, bias=offset[:, t : t + 1], scale=factor[:, t : t + 1]
+            )
 
         uv_first = sb.tile([PARTS, 2, 2, S], F32, name="uv_first", tag="w1_codes", align_bytes=64)
-        u_second = sb.tile([PARTS, 2, S], F32, name="u_second", tag="w2_dealt", align_bytes=64)
-        v_second = sb.tile([PARTS, 2, S], F32, name="v_second", tag="e_word_table")
+        u_second = sb.tile([PARTS, 2, S], F32, name="u_second", tag="e_word_table")
         u = [uv_first[:, 0, :, :], u_second[:]]
-        v = [uv_first[:, 1, :, :], v_second[:]]
-        for out, factor, offset in ((u[0], c3, c2), (v[0], c1, c0)):
+        for n, (factor, offset) in enumerate(((c3, c2), (c1, c0))):
             for t in range(2):
-                nc.scalar.activation(
-                    out[:, t, :], a[:, t, :], ACT.Identity, bias=offset[:, t : t + 1], scale=factor[:, t : t + 1]
-                )
-        for engine, out, factor, offset in ((nc.gpsimd, u[1], c3, c2), (nc.vector, v[1], c1, c0)):
-            for t in range(2, PACK):
-                engine.tensor_scalar(
-                    out[:, t - 2, :], a[:, t, :], factor[:, t : t + 1], offset[:, t : t + 1], ALU.mult, ALU.add
-                )
+                affine_on_scalar(uv_first[:, n, t, :], t, slice(0, S), factor, offset)
+        for t in range(2, PACK):
+            nc.vector.tensor_scalar(
+                u_second[:, t - 2, :], a[:, t, :], c3[:, t : t + 1], c2[:, t : t + 1], ALU.mult, ALU.add
+            )
 
-        item_coordinate(1)
+        v_second = []
+        for h, groups, banks in ((0, ((0, 2), (2, 4)), (4, 5)), (1, ((0, 2), (2, 4)), (6, 7))):
+            item_coordinate(h, groups, banks)
+            v_half = sb.tile([PARTS, 2, HALF], F32, name="v_second%d" % h, tag="e_picked%d" % h, align_bytes=64)
+            for t in range(2, PACK):
+                affine_on_scalar(v_half[:, t - 2, :], t, halves[h], c1, c0)
+            v_second.append(v_half)
+
+        def v_part(pair, cols):
+            if pair == 0:
+                return uv_first[:, 1, :, cols]
+            h = cols.start // HALF
+            return v_second[h][:, :, cols.start - h * HALF : cols.stop - h * HALF]
 
         y_rows = out_0.rearrange("(p t) s -> p t s", t=PACK)
         y_words = out_1[0].rearrange("p c r -> p (c r)").bitcast(I32)
@@ -184,7 +197,6 @@ def tile_picked_ylatt_lin_po_kernel(
         y_codes = sb.tile([PARTS, S], U32, name="y_codes", align_bytes=64)
         y_plane = sb.tile([PARTS, S], U8, name="y_plane", align_bytes=64)
         pairs = [slice(0, 2), slice(2, 4)]
-        halves = [slice(0, HALF), slice(HALF, S)]
         chunks = [slice(first, first + width) for first, width in CHUNKS]
 
         def multiply(pair, cols):
@@ -193,7 +205,7 @@ def tile_picked_ylatt_lin_po_kernel(
 
         def add(pair, cols):
             ts = pairs[pair]
-            nc.vector.tensor_tensor(y[:, ts, cols], up[:, ts, cols], v[pair][:, :, cols], ALU.add)
+            nc.vector.tensor_tensor(y[:, ts, cols], up[:, ts, cols], v_part(pair, cols), ALU.add)
 
         def store_rows(ts, cols):
             nc.sync.dma_start(out=y_rows[:, ts, cols], in_=y[:, ts, cols])

@@ -60,11 +60,6 @@ def tile_picked_ylatt_lin_po_kernel(
         nc.gpsimd.memset(x_scale_table[:].bitcast(I32), 0)
         nc.gpsimd.memset(e_scale_table[:].bitcast(I32), 0)
 
-        warm_in = sb.tile([PARTS, 1], F32, name="warm_in")
-        warm_out = sb.tile([PARTS, 1], F32, name="warm_out")
-        nc.vector.memset(warm_in[:], 0.0)
-        nc.scalar.activation(warm_out[:], warm_in[:], ACT.Sigmoid)
-
         nc.gpsimd.dma_start(out=theta_sb[:], in_=theta.rearrange("(p t) c -> p t c", t=PACK))
         load_words(x_word_table, x_words)
         nc.sync.dma_start(offs_sb[:], offs)

@@ -21,7 +21,7 @@ HALF = 256
 PER_COLUMN = 16
 FLOPS = 2 * 2 * K * M * S
 
-SCALAR_SHARE = 80
+SCALAR_SHARE = 336
 
 CHUNKS = ((0, 256), (256, 128), (384, 128))
 
@@ -35,6 +35,7 @@ def tile_picked_ylatt_lin_po_kernel(
 
     with ExitStack() as ctx:
         sb = ctx.enter_context(tc.tile_pool(name="sb", bufs=1))
+        placed = ctx.enter_context(tc.tile_pool(name="placed", bufs=1))
         ps = ctx.enter_context(tc.psum_pool(name="ps", bufs=1))
 
         offs_sb = sb.tile([PARTS, S // PER_COLUMN], U16, name="offs_sb")
@@ -44,8 +45,8 @@ def tile_picked_ylatt_lin_po_kernel(
         x_scale_table = sb.tile([PARTS, users], U8, name="x_scale_table")
         e_scale_table = sb.tile([PARTS, items], U8, name="e_scale_table")
         theta_sb = sb.tile([PARTS, PACK, 4], F32, name="theta_sb")
-        w1_raw = [sb.tile([PARTS, PACK, HALF], F32, name="w1_raw%d" % h) for h in range(2)]
-        w2_raw = sb.tile([PARTS, PACK, M], F32, name="w2_raw")
+        w1_raw = sb.tile([PARTS, PACK, M], F32, name="w1_raw")
+        w2_raw = sb.tile([PARTS, PACK, M], F32, name="w2_raw", tag="w2_raw")
 
         def load_words(table, words):
             nc.sync.dma_start(out=table[:], in_=words[0].rearrange("p c r -> p (c r)").bitcast(I32))
@@ -59,42 +60,47 @@ def tile_picked_ylatt_lin_po_kernel(
 
         nc.gpsimd.memset(x_scale_table[:].bitcast(I32), 0)
         nc.gpsimd.memset(e_scale_table[:].bitcast(I32), 0)
+        e_plane = sb.tile([PARTS, S], U8, name="e_plane", align_bytes=64)
+        nc.gpsimd.memset(e_plane[:].bitcast(I32), 0)
 
         nc.gpsimd.dma_start(out=theta_sb[:], in_=theta.rearrange("(p t) c -> p t c", t=PACK))
         load_words(x_word_table, x_words)
         nc.sync.dma_start(offs_sb[:], offs)
         load_scales(x_scale_table, x_scales, 0)
-        w1_rows = w1.rearrange("(p j) m -> p j m", j=PACK)
-        for h in range(2):
-            nc.sync.dma_start(out=w1_raw[h][:], in_=w1_rows[:, :, h * HALF : (h + 1) * HALF])
+        nc.sync.dma_start(out=w1_raw[:], in_=w1.rearrange("(p j) m -> p j m", j=PACK))
         nc.sync.dma_start(item_sb[:], item)
-        load_scales(e_scale_table, e_scales, 4)
+        nc.sync.dma_start(out=e_scale_table[4:PARTS:8, :].bitcast(I32), in_=e_scales[0].bitcast(I32))
         nc.sync.dma_start(out=w2_raw[:], in_=w2.rearrange("(p j) m -> p j m", j=PACK))
         load_words(e_word_table, e_words)
 
-        c0 = theta_sb[:, :, 0]
-        c1 = sb.tile([PARTS, PACK], F32, name="c1")
-        c2 = sb.tile([PARTS, PACK], F32, name="c2")
-        theta3_less_theta2 = sb.tile([PARTS, PACK], F32, name="theta3_less_theta2")
-        c3 = sb.tile([PARTS, PACK], F32, name="c3")
-        nc.gpsimd.tensor_tensor(c1[:], theta_sb[:, :, 1], c0, ALU.subtract)
-        nc.gpsimd.tensor_tensor(c2[:], theta_sb[:, :, 2], c0, ALU.subtract)
-        nc.gpsimd.tensor_tensor(theta3_less_theta2[:], theta_sb[:, :, 3], theta_sb[:, :, 2], ALU.subtract)
-        nc.gpsimd.tensor_tensor(c3[:], theta3_less_theta2[:], c1[:], ALU.subtract)
+        quarter = sb.tile([PARTS, PACK, 2, 2], F32, name="quarter")
+        along_a = sb.tile([PARTS, 2, PACK, 2], F32, name="along_a")
+        v_terms = sb.tile([PARTS, 2, PACK], F32, name="v_terms")
+        u_terms = sb.tile([PARTS, 2, PACK], F32, name="u_terms")
+        nc.gpsimd.tensor_scalar(
+            quarter[:].rearrange("p t b a -> p (t b a)"), theta_sb[:].rearrange("p t c -> p (t c)"), 0.25, 0.0, ALU.mult, ALU.add
+        )
+        nc.gpsimd.tensor_tensor(along_a[:, 0, :, :], quarter[:, :, :, 1], quarter[:, :, :, 0], ALU.add)
+        nc.gpsimd.tensor_tensor(along_a[:, 1, :, :], quarter[:, :, :, 1], quarter[:, :, :, 0], ALU.subtract)
+        nc.gpsimd.tensor_tensor(v_terms[:], along_a[:, :, :, 1], along_a[:, :, :, 0], ALU.add)
+        nc.gpsimd.tensor_tensor(u_terms[:], along_a[:, :, :, 1], along_a[:, :, :, 0], ALU.subtract)
+        c0, c1 = v_terms[:, 0, :], v_terms[:, 1, :]
+        c2, c3 = u_terms[:, 0, :], u_terms[:, 1, :]
 
         dealt = {}
         codes = {}
         planes = {}
+        dealt["w1"] = sb.tile([PARTS, PACK, PARTS, PACK], BF16, name="w1_dealt", align_bytes=64)
+        dealt["w2"] = placed.tile([PARTS, PACK, PARTS, PACK], BF16, name="w2_dealt", align_bytes=64, offset=6144)
         for w in ("w1", "w2"):
-            dealt[w] = sb.tile([PARTS, PACK, PARTS, PACK], BF16, name=w + "_dealt", tag=w + "_dealt", align_bytes=64)
             codes[w] = sb.tile([PARTS, M], U32, name=w + "_codes", tag=w + "_codes", align_bytes=64)
             planes[w] = sb.tile([PARTS, M], U8, name=w + "_plane", align_bytes=64)
 
-        def deal_weight(copy, w, raw, first_column):
+        def deal_weight(copy, w, raw, first_column, t0=0, t1=PACK):
             m0 = first_column // PACK
             copy(
-                out=dealt[w][:, :, m0 : m0 + raw.shape[2] // PACK, :].rearrange("p t m j -> p m j t"),
-                in_=raw.rearrange("p j (m t) -> p m j t", t=PACK),
+                out=dealt[w][:, t0:t1, m0 : m0 + raw.shape[2] // PACK, :].rearrange("p t m j -> p m j t"),
+                in_=raw.rearrange("p j (m t) -> p m j t", t=PACK)[:, :, :, t0:t1],
             )
 
         def quantize_weight(w, t0, t1):
@@ -119,23 +125,30 @@ def tile_picked_ylatt_lin_po_kernel(
         x_plane = sb.tile([PARTS, S], U8, name="x_plane", align_bytes=64)
         nc.vector.tensor_copy(x_picked[:], x_word_table[:].bitcast(U32).indirect(offs_sb[:]))
         nc.vector.tensor_copy(x_plane[:], x_scale_table[:].indirect(offs_sb[:]))
-        deal_weight(nc.scalar.copy, "w1", w1_raw[0][:], 0)
-        deal_weight(nc.scalar.copy, "w1", w1_raw[1][:, :, :SCALAR_SHARE], HALF)
-        deal_weight(nc.vector.tensor_copy, "w1", w1_raw[1][:, :, SCALAR_SHARE:], HALF + SCALAR_SHARE)
+        deal_weight(nc.scalar.copy, "w1", w1_raw[:, :, :SCALAR_SHARE], 0)
+        deal_weight(nc.vector.tensor_copy, "w1", w1_raw[:, :, SCALAR_SHARE:], SCALAR_SHARE)
+        e_rows = sb.tile([PARTS, S], U8, name="e_rows", align_bytes=64)
+        nc.vector.tensor_copy(e_rows[:], e_scale_table[:].indirect(item_sb[:]))
+        for r in range(4):
+            nc.scalar.dma_start(
+                out=e_plane[4 + r : PARTS : 32, :].bitcast(I32),
+                in_=e_rows[4 + 8 * r : PARTS : 32, :].bitcast(I32),
+            )
         for t in range(PACK):
             quantize_weight("w1", t, t + 1)
         a = sb.tile([PARTS, PACK, S], F32, name="a")
         for t in range(PACK):
             acc_a = ps.tile([PARTS, S], F32, name="acc_a%d" % t, tag="bank%d" % t)
             product(acc_a[:], "w1", t, x_picked[:], x_plane[:])
-            nc.scalar.activation(a[:, t, :], acc_a[:], ACT.Sigmoid)
+            nc.scalar.activation(a[:, t, :], acc_a[:], ACT.Tanh, scale=0.5)
 
-        e_plane = sb.tile([PARTS, S], U8, name="e_plane", align_bytes=64)
-        nc.vector.tensor_copy(e_plane[:], e_scale_table[:].indirect(item_sb[:]))
-        deal_weight(nc.vector.tensor_copy, "w2", w2_raw[:], 0)
-        quantize_weight("w2", 0, PACK)
+        for t0 in (0, 2):
+            deal_weight(nc.vector.tensor_copy, "w2", w2_raw[:], 0, t0, t0 + 2)
+        for t0 in (0, 2):
+            quantize_weight("w2", t0, t0 + 2)
+        picked_at = (6208, 9280)
         e_picked = [
-            sb.tile([PARTS, HALF], U32, name="e_picked%d" % h, tag="e_picked%d" % h, align_bytes=64) for h in range(2)
+            placed.tile([PARTS, HALF], U32, name="e_picked%d" % h, align_bytes=64, offset=picked_at[h]) for h in range(2)
         ]
         for h in range(2):
             offsets = item_sb[:, h * HALF // PER_COLUMN : (h + 1) * HALF // PER_COLUMN]
@@ -149,37 +162,36 @@ def tile_picked_ylatt_lin_po_kernel(
                 acc_p = ps.tile([PARTS, t1 - t0, HALF], F32, name="acc_p%d%d" % (h, t0), tag="bank%d" % bank)
                 for t in range(t0, t1):
                     product(acc_p[:, t - t0, :], "w2", t, e_picked[h][:], e_plane[4:, halves[h]])
-                nc.scalar.activation(p[:, t0:t1, halves[h]], acc_p[:], ACT.Sigmoid)
+                nc.scalar.activation(p[:, t0:t1, halves[h]], acc_p[:], ACT.Tanh, scale=0.5)
 
         def affine_on_scalar(out, t, cols, factor, offset):
             nc.scalar.activation(
                 out, a[:, t, cols], ACT.Identity, bias=offset[:, t : t + 1], scale=factor[:, t : t + 1]
             )
 
-        uv_first = sb.tile([PARTS, 2, 2, S], F32, name="uv_first", tag="w1_codes", align_bytes=64)
-        u_second = sb.tile([PARTS, 2, S], F32, name="u_second", tag="e_word_table")
-        u = [uv_first[:, 0, :, :], u_second[:]]
-        for n, (factor, offset) in enumerate(((c3, c2), (c1, c0))):
-            for t in range(2):
-                affine_on_scalar(uv_first[:, n, t, :], t, slice(0, S), factor, offset)
-        for t in range(2, PACK):
-            nc.vector.tensor_scalar(
-                u_second[:, t - 2, :], a[:, t, :], c3[:, t : t + 1], c2[:, t : t + 1], ALU.mult, ALU.add
+        u_first = sb.tile([PARTS, 2, S], F32, name="u_first", tag="w1_codes", align_bytes=64)
+        on_gpsimd = placed.tile([PARTS, 3, S], F32, name="on_gpsimd", align_bytes=64, offset=64)
+        u = [u_first[:], on_gpsimd[:, 1:3, :]]
+        for t in range(2):
+            affine_on_scalar(u_first[:, t, :], t, slice(0, S), c3, c2)
+        for n, (t, factor, offset) in enumerate(((0, c1, c0), (2, c3, c2), (3, c3, c2))):
+            nc.gpsimd.tensor_scalar(
+                on_gpsimd[:, n, :], a[:, t, :], factor[:, t : t + 1], offset[:, t : t + 1], ALU.mult, ALU.add
             )
 
         v_second = []
-        for h, groups, banks in ((0, ((0, 2), (2, 4)), (4, 5)), (1, ((0, 2), (2, 4)), (6, 7))):
+        for h, groups, banks in ((0, ((0, 1), (1, 2), (2, 4)), (4, 5, 6)), (1, ((0, 2), (2, 4)), (7, 0))):
             item_coordinate(h, groups, banks)
-            v_half = sb.tile([PARTS, 2, HALF], F32, name="v_second%d" % h, tag="e_picked%d" % h, align_bytes=64)
-            for t in range(2, PACK):
-                affine_on_scalar(v_half[:, t - 2, :], t, halves[h], c1, c0)
+            v_half = placed.tile([PARTS, 3, HALF], F32, name="v_second%d" % h, align_bytes=64, offset=picked_at[h])
+            for t in range(1, PACK):
+                affine_on_scalar(v_half[:, t - 1, :], t, halves[h], c1, c0)
             v_second.append(v_half)
 
-        def v_part(pair, cols):
-            if pair == 0:
-                return uv_first[:, 1, :, cols]
+        def v_part(t0, t1, cols):
+            if t0 == 0:
+                return on_gpsimd[:, 0:1, cols]
             h = cols.start // HALF
-            return v_second[h][:, :, cols.start - h * HALF : cols.stop - h * HALF]
+            return v_second[h][:, t0 - 1 : t1 - 1, cols.start - h * HALF : cols.stop - h * HALF]
 
         y_rows = out_0.rearrange("(p t) s -> p t s", t=PACK)
         y_words = out_1[0].rearrange("p c r -> p (c r)").bitcast(I32)
@@ -198,9 +210,8 @@ def tile_picked_ylatt_lin_po_kernel(
             ts = pairs[pair]
             nc.vector.tensor_tensor(up[:, ts, cols], u[pair][:, :, cols], p[:, ts, cols], ALU.mult)
 
-        def add(pair, cols):
-            ts = pairs[pair]
-            nc.vector.tensor_tensor(y[:, ts, cols], up[:, ts, cols], v_part(pair, cols), ALU.add)
+        def add(t0, t1, cols):
+            nc.vector.tensor_tensor(y[:, t0:t1, cols], up[:, t0:t1, cols], v_part(t0, t1, cols), ALU.add)
 
         def store_rows(ts, cols):
             nc.sync.dma_start(out=y_rows[:, ts, cols], in_=y[:, ts, cols])
@@ -221,20 +232,26 @@ def tile_picked_ylatt_lin_po_kernel(
         def store_words(cols):
             nc.sync.dma_start(out=y_words[:, cols], in_=y_codes[:, cols].bitcast(I32))
 
-        for pair in range(2):
-            multiply(pair, halves[0])
-        for pair in range(2):
-            add(pair, halves[0])
+        def multiply_slice(t, cols):
+            nc.vector.tensor_tensor(up[:, t, cols], u_first[:, t, cols], p[:, t, cols], ALU.mult)
+
+        multiply_slice(0, halves[0])
+        multiply_slice(1, halves[0])
+        add(0, 1, halves[0])
+        multiply(1, halves[0])
+        add(1, 2, halves[0])
+        add(2, 4, halves[0])
         store_rows(slice(0, PACK), halves[0])
         group_result(nc.scalar.copy, 0)
 
         for pair in range(2):
             multiply(pair, halves[1])
-        add(0, halves[1])
+        add(0, 1, halves[1])
+        add(1, 2, halves[1])
         store_rows(pairs[0], halves[1])
-        add(1, chunks[1])
+        add(2, 4, chunks[1])
         group_result(nc.scalar.copy, 1)
-        add(1, chunks[2])
+        add(2, 4, chunks[2])
         store_rows(pairs[1], halves[1])
 
         quantize_result(0)

@@ -21,7 +21,7 @@ HALF = 256
 PER_COLUMN = 16
 FLOPS = 2 * 2 * K * M * S
 
-SCALAR_SHARE = 336
+SCALAR_SHARE = 272
 
 CHUNKS = ((0, 256), (256, 128), (384, 128))
 
@@ -45,7 +45,7 @@ def tile_picked_ylatt_lin_po_kernel(
         x_scale_table = sb.tile([PARTS, users], U8, name="x_scale_table")
         e_scale_table = sb.tile([PARTS, items], U8, name="e_scale_table")
         theta_sb = sb.tile([PARTS, PACK, 4], F32, name="theta_sb")
-        w1_raw = sb.tile([PARTS, PACK, M], F32, name="w1_raw")
+        w1_raw = sb.tile([PARTS, PACK, M], F32, name="w1_raw", tag="w1_raw")
         w2_raw = sb.tile([PARTS, PACK, M], F32, name="w2_raw", tag="w2_raw")
 
         def load_words(table, words):
@@ -72,20 +72,6 @@ def tile_picked_ylatt_lin_po_kernel(
         nc.sync.dma_start(out=e_scale_table[4:PARTS:8, :].bitcast(I32), in_=e_scales[0].bitcast(I32))
         nc.sync.dma_start(out=w2_raw[:], in_=w2.rearrange("(p j) m -> p j m", j=PACK))
         load_words(e_word_table, e_words)
-
-        quarter = sb.tile([PARTS, PACK, 2, 2], F32, name="quarter")
-        along_a = sb.tile([PARTS, 2, PACK, 2], F32, name="along_a")
-        v_terms = sb.tile([PARTS, 2, PACK], F32, name="v_terms")
-        u_terms = sb.tile([PARTS, 2, PACK], F32, name="u_terms")
-        nc.gpsimd.tensor_scalar(
-            quarter[:].rearrange("p t b a -> p (t b a)"), theta_sb[:].rearrange("p t c -> p (t c)"), 0.25, 0.0, ALU.mult, ALU.add
-        )
-        nc.gpsimd.tensor_tensor(along_a[:, 0, :, :], quarter[:, :, :, 1], quarter[:, :, :, 0], ALU.add)
-        nc.gpsimd.tensor_tensor(along_a[:, 1, :, :], quarter[:, :, :, 1], quarter[:, :, :, 0], ALU.subtract)
-        nc.gpsimd.tensor_tensor(v_terms[:], along_a[:, :, :, 1], along_a[:, :, :, 0], ALU.add)
-        nc.gpsimd.tensor_tensor(u_terms[:], along_a[:, :, :, 1], along_a[:, :, :, 0], ALU.subtract)
-        c0, c1 = v_terms[:, 0, :], v_terms[:, 1, :]
-        c2, c3 = u_terms[:, 0, :], u_terms[:, 1, :]
 
         dealt = {}
         codes = {}
@@ -126,7 +112,14 @@ def tile_picked_ylatt_lin_po_kernel(
         nc.vector.tensor_copy(x_picked[:], x_word_table[:].bitcast(U32).indirect(offs_sb[:]))
         nc.vector.tensor_copy(x_plane[:], x_scale_table[:].indirect(offs_sb[:]))
         deal_weight(nc.scalar.copy, "w1", w1_raw[:, :, :SCALAR_SHARE], 0)
-        deal_weight(nc.vector.tensor_copy, "w1", w1_raw[:, :, SCALAR_SHARE:], SCALAR_SHARE)
+        nc.gpsimd.tensor_scalar(
+            dealt["w1"][:, :, SCALAR_SHARE // PACK :, :].rearrange("p t m j -> p m t j"),
+            w1_raw[:, :, SCALAR_SHARE:].rearrange("p j (m t) -> p m t j", t=PACK),
+            1.0,
+            0.0,
+            ALU.mult,
+            ALU.add,
+        )
         e_rows = sb.tile([PARTS, S], U8, name="e_rows", align_bytes=64)
         nc.vector.tensor_copy(e_rows[:], e_scale_table[:].indirect(item_sb[:]))
         for r in range(4):
@@ -134,8 +127,22 @@ def tile_picked_ylatt_lin_po_kernel(
                 out=e_plane[4 + r : PARTS : 32, :].bitcast(I32),
                 in_=e_rows[4 + 8 * r : PARTS : 32, :].bitcast(I32),
             )
-        for t in range(PACK):
-            quantize_weight("w1", t, t + 1)
+        quarter = sb.tile([PARTS, PACK, 2, 2], F32, name="quarter", tag="w1_raw")
+        along_a = sb.tile([PARTS, 2, PACK, 2], F32, name="along_a")
+        v_terms = sb.tile([PARTS, 2, PACK], F32, name="v_terms")
+        u_terms = sb.tile([PARTS, 2, PACK], F32, name="u_terms")
+        c0, c1 = v_terms[:, 0, :], v_terms[:, 1, :]
+        c2, c3 = u_terms[:, 0, :], u_terms[:, 1, :]
+        quantize_weight("w1", 0, 1)
+        nc.vector.tensor_scalar(
+            quarter[:].rearrange("p t b a -> p (t b a)"), theta_sb[:].rearrange("p t c -> p (t c)"), 0.25, None, ALU.mult
+        )
+        quantize_weight("w1", 1, 2)
+        nc.vector.tensor_tensor(along_a[:, 0, :, :], quarter[:, :, :, 1], quarter[:, :, :, 0], ALU.add)
+        nc.vector.tensor_tensor(along_a[:, 1, :, :], quarter[:, :, :, 1], quarter[:, :, :, 0], ALU.subtract)
+        quantize_weight("w1", 2, PACK)
+        nc.vector.tensor_tensor(v_terms[:], along_a[:, :, :, 1], along_a[:, :, :, 0], ALU.add)
+        nc.vector.tensor_tensor(u_terms[:], along_a[:, :, :, 1], along_a[:, :, :, 0], ALU.subtract)
         a = sb.tile([PARTS, PACK, S], F32, name="a")
         for t in range(PACK):
             acc_a = ps.tile([PARTS, S], F32, name="acc_a%d" % t, tag="bank%d" % t)

@@ -176,15 +176,17 @@ def tile_picked_ylatt_lin_po_kernel(
                 out, a[:, t, cols], ACT.Identity, bias=offset[:, t : t + 1], scale=factor[:, t : t + 1]
             )
 
-        u_first = sb.tile([PARTS, 2, S], F32, name="u_first", tag="w1_codes", align_bytes=64)
-        on_gpsimd = placed.tile([PARTS, 3, S], F32, name="on_gpsimd", align_bytes=64, offset=64)
-        u = [u_first[:], on_gpsimd[:, 1:3, :]]
+        u_first = placed.tile([PARTS, 2, S], F32, name="u_first", align_bytes=64, offset=2112)
+        u_second = sb.tile([PARTS, 2, S], F32, name="u_second", tag="w1_codes", align_bytes=64)
+        v_first = sb.tile([PARTS, 1, S], F32, name="v_first", tag="e_word_table")
+        u = [u_first[:], u_second[:]]
         for t in range(2):
-            affine_on_scalar(u_first[:, t, :], t, slice(0, S), c3, c2)
-        for n, (t, factor, offset) in enumerate(((0, c1, c0), (2, c3, c2), (3, c3, c2))):
             nc.gpsimd.tensor_scalar(
-                on_gpsimd[:, n, :], a[:, t, :], factor[:, t : t + 1], offset[:, t : t + 1], ALU.mult, ALU.add
+                u_first[:, t, :], a[:, t, :], c3[:, t : t + 1], c2[:, t : t + 1], ALU.mult, ALU.add
             )
+        for t in range(2, PACK):
+            affine_on_scalar(u_second[:, t - 2, :], t, slice(0, S), c3, c2)
+        nc.vector.tensor_scalar(v_first[:, 0, :], a[:, 0, :], c1[:, 0:1], c0[:, 0:1], ALU.mult, ALU.add)
 
         v_second = []
         for h, groups, banks in ((0, ((0, 1), (1, 2), (2, 4)), (4, 5, 6)), (1, ((0, 2), (2, 4)), (7, 0))):
@@ -196,7 +198,7 @@ def tile_picked_ylatt_lin_po_kernel(
 
         def v_part(t0, t1, cols):
             if t0 == 0:
-                return on_gpsimd[:, 0:1, cols]
+                return v_first[:, :, cols]
             h = cols.start // HALF
             return v_second[h][:, t0 - 1 : t1 - 1, cols.start - h * HALF : cols.stop - h * HALF]
 

@@ -18,6 +18,7 @@ K = 512
 M = 512
 S = 512
 HALF = 256
+QUARTER = 128
 PER_COLUMN = 16
 FLOPS = 2 * 2 * K * M * S
 
@@ -151,12 +152,15 @@ def tile_picked_ylatt_lin_po_kernel(
 
         for t0 in (0, 2):
             deal_weight(nc.vector.tensor_copy, "w2", w2_raw[:], 0, t0, t0 + 2)
+        v_first = sb.tile([PARTS, 1, S], F32, name="v_first", tag="w2_raw")
+        nc.vector.tensor_scalar(v_first[:, 0, :], a[:, 0, :], c1[:, 0:1], c0[:, 0:1], ALU.mult, ALU.add)
         for t0 in (0, 2):
             quantize_weight("w2", t0, t0 + 2)
         picked_at = (6208, 9280)
         e_picked = [
             placed.tile([PARTS, HALF], U32, name="e_picked%d" % h, align_bytes=64, offset=picked_at[h]) for h in range(2)
         ]
+        stretches = [slice(0, QUARTER), slice(QUARTER, HALF), slice(HALF, S)]
         for h in range(2):
             offsets = item_sb[:, h * HALF // PER_COLUMN : (h + 1) * HALF // PER_COLUMN]
             nc.vector.tensor_copy(e_picked[h][:], e_word_table[:].bitcast(U32).indirect(offsets))
@@ -164,12 +168,14 @@ def tile_picked_ylatt_lin_po_kernel(
 
         halves = [slice(0, HALF), slice(HALF, S)]
 
-        def item_coordinate(h, groups, banks):
-            for (t0, t1), bank in zip(groups, banks):
-                acc_p = ps.tile([PARTS, t1 - t0, HALF], F32, name="acc_p%d%d" % (h, t0), tag="bank%d" % bank)
-                for t in range(t0, t1):
-                    product(acc_p[:, t - t0, :], "w2", t, e_picked[h][:], e_plane[4:, halves[h]])
-                nc.scalar.activation(p[:, t0:t1, halves[h]], acc_p[:], ACT.Tanh, scale=0.5)
+        def item_coordinate(cols, banks):
+            h = cols.start // HALF
+            picked = e_picked[h][:, cols.start - h * HALF : cols.stop - h * HALF]
+            for t0, bank in zip((0, 2), banks):
+                acc_p = ps.tile([PARTS, 2, cols.stop - cols.start], F32, name="acc_p%d" % bank, tag="bank%d" % bank)
+                for t in range(t0, t0 + 2):
+                    product(acc_p[:, t - t0, :], "w2", t, picked, e_plane[4:, cols])
+                nc.scalar.activation(p[:, t0 : t0 + 2, cols], acc_p[:], ACT.Tanh, scale=0.5)
 
         def affine_on_scalar(out, t, cols, factor, offset):
             nc.scalar.activation(
@@ -178,7 +184,6 @@ def tile_picked_ylatt_lin_po_kernel(
 
         u_first = placed.tile([PARTS, 2, S], F32, name="u_first", align_bytes=64, offset=2112)
         u_second = sb.tile([PARTS, 2, S], F32, name="u_second", tag="w1_codes", align_bytes=64)
-        v_first = sb.tile([PARTS, 1, S], F32, name="v_first", tag="e_word_table")
         u = [u_first[:], u_second[:]]
         for t in range(2):
             nc.gpsimd.tensor_scalar(
@@ -186,11 +191,11 @@ def tile_picked_ylatt_lin_po_kernel(
             )
         for t in range(2, PACK):
             affine_on_scalar(u_second[:, t - 2, :], t, slice(0, S), c3, c2)
-        nc.vector.tensor_scalar(v_first[:, 0, :], a[:, 0, :], c1[:, 0:1], c0[:, 0:1], ALU.mult, ALU.add)
 
         v_second = []
-        for h, groups, banks in ((0, ((0, 1), (1, 2), (2, 4)), (4, 5, 6)), (1, ((0, 2), (2, 4)), (7, 0))):
-            item_coordinate(h, groups, banks)
+        item_coordinate(stretches[0], (4, 5))
+        for h, banks in ((0, (6, 7)), (1, (0, 1))):
+            item_coordinate(stretches[h + 1], banks)
             v_half = placed.tile([PARTS, 3, HALF], F32, name="v_second%d" % h, align_bytes=64, offset=picked_at[h])
             for t in range(1, PACK):
                 affine_on_scalar(v_half[:, t - 1, :], t, halves[h], c1, c0)
@@ -241,13 +246,10 @@ def tile_picked_ylatt_lin_po_kernel(
         def store_words(cols):
             nc.sync.dma_start(out=y_words[:, cols], in_=y_codes[:, cols].bitcast(I32))
 
-        def multiply_slice(t, cols):
-            nc.vector.tensor_tensor(up[:, t, cols], u_first[:, t, cols], p[:, t, cols], ALU.mult)
-
-        multiply_slice(0, halves[0])
-        multiply_slice(1, halves[0])
+        for cols in stretches[:2]:
+            for pair in range(2):
+                multiply(pair, cols)
         add(0, 1, halves[0])
-        multiply(1, halves[0])
         add(1, 2, halves[0])
         add(2, 4, halves[0])
         store_rows(slice(0, PACK), halves[0])

@@ -22,7 +22,7 @@ QUARTER = 128
 PER_COLUMN = 16
 FLOPS = 2 * 2 * K * M * S
 
-SCALAR_SHARE = 272
+SCALAR_SHARE = 304
 
 CHUNKS = ((0, 256), (256, 128), (384, 128))
 
@@ -152,7 +152,7 @@ def tile_picked_ylatt_lin_po_kernel(
 
         for t0 in (0, 2):
             deal_weight(nc.vector.tensor_copy, "w2", w2_raw[:], 0, t0, t0 + 2)
-        v_first = sb.tile([PARTS, 1, S], F32, name="v_first", tag="w2_raw")
+        v_first = sb.tile([PARTS, 2, S], F32, name="v_first", tag="w2_raw")
         nc.vector.tensor_scalar(v_first[:, 0, :], a[:, 0, :], c1[:, 0:1], c0[:, 0:1], ALU.mult, ALU.add)
         for t0 in (0, 2):
             quantize_weight("w2", t0, t0 + 2)
@@ -183,29 +183,32 @@ def tile_picked_ylatt_lin_po_kernel(
             )
 
         u_first = placed.tile([PARTS, 2, S], F32, name="u_first", align_bytes=64, offset=2112)
-        u_second = sb.tile([PARTS, 2, S], F32, name="u_second", tag="w1_codes", align_bytes=64)
+        u_second = sb.tile([PARTS, 2, S], F32, name="u_second", tag="e_word_table")
         u = [u_first[:], u_second[:]]
         for t in range(2):
             nc.gpsimd.tensor_scalar(
                 u_first[:, t, :], a[:, t, :], c3[:, t : t + 1], c2[:, t : t + 1], ALU.mult, ALU.add
             )
+        affine_on_scalar(v_first[:, 1, :], 1, slice(0, S), c1, c0)
         for t in range(2, PACK):
-            affine_on_scalar(u_second[:, t - 2, :], t, slice(0, S), c3, c2)
+            nc.vector.tensor_scalar(
+                u_second[:, t - 2, :], a[:, t, :], c3[:, t : t + 1], c2[:, t : t + 1], ALU.mult, ALU.add
+            )
 
         v_second = []
         item_coordinate(stretches[0], (4, 5))
         for h, banks in ((0, (6, 7)), (1, (0, 1))):
             item_coordinate(stretches[h + 1], banks)
-            v_half = placed.tile([PARTS, 3, HALF], F32, name="v_second%d" % h, align_bytes=64, offset=picked_at[h])
-            for t in range(1, PACK):
-                affine_on_scalar(v_half[:, t - 1, :], t, halves[h], c1, c0)
+            v_half = placed.tile([PARTS, 2, HALF], F32, name="v_second%d" % h, align_bytes=64, offset=picked_at[h])
+            for t in range(2, PACK):
+                affine_on_scalar(v_half[:, t - 2, :], t, halves[h], c1, c0)
             v_second.append(v_half)
 
         def v_part(t0, t1, cols):
-            if t0 == 0:
-                return v_first[:, :, cols]
+            if t0 < 2:
+                return v_first[:, t0:t1, cols]
             h = cols.start // HALF
-            return v_second[h][:, t0 - 1 : t1 - 1, cols.start - h * HALF : cols.stop - h * HALF]
+            return v_second[h][:, t0 - 2 : t1 - 2, cols.start - h * HALF : cols.stop - h * HALF]
 
         y_rows = out_0.rearrange("(p t) s -> p t s", t=PACK)
         y_words = out_1[0].rearrange("p c r -> p (c r)").bitcast(I32)
@@ -249,16 +252,14 @@ def tile_picked_ylatt_lin_po_kernel(
         for cols in stretches[:2]:
             for pair in range(2):
                 multiply(pair, cols)
-        add(0, 1, halves[0])
-        add(1, 2, halves[0])
+        add(0, 2, halves[0])
         add(2, 4, halves[0])
         store_rows(slice(0, PACK), halves[0])
         group_result(nc.scalar.copy, 0)
 
         for pair in range(2):
             multiply(pair, halves[1])
-        add(0, 1, halves[1])
-        add(1, 2, halves[1])
+        add(0, 2, halves[1])
         store_rows(pairs[0], halves[1])
         add(2, 4, chunks[1])
         group_result(nc.scalar.copy, 1)

@@ -152,8 +152,8 @@ def tile_picked_ylatt_lin_po_kernel(
 
         for t0 in (0, 2):
             deal_weight(nc.vector.tensor_copy, "w2", w2_raw[:], 0, t0, t0 + 2)
-        v_first = sb.tile([PARTS, 2, S], F32, name="v_first", tag="w2_raw")
-        nc.vector.tensor_scalar(v_first[:, 0, :], a[:, 0, :], c1[:, 0:1], c0[:, 0:1], ALU.mult, ALU.add)
+        u_first = sb.tile([PARTS, 2, S], F32, name="u_first", tag="w2_raw")
+        nc.vector.tensor_scalar(u_first[:, 0, :], a[:, 0, :], c3[:, 0:1], c2[:, 0:1], ALU.mult, ALU.add)
         for t0 in (0, 2):
             quantize_weight("w2", t0, t0 + 2)
         picked_at = (6208, 9280)
@@ -182,14 +182,14 @@ def tile_picked_ylatt_lin_po_kernel(
                 out, a[:, t, cols], ACT.Identity, bias=offset[:, t : t + 1], scale=factor[:, t : t + 1]
             )
 
-        u_first = placed.tile([PARTS, 2, S], F32, name="u_first", align_bytes=64, offset=2112)
+        v_first = placed.tile([PARTS, 2, S], F32, name="v_first", align_bytes=64, offset=2112)
         u_second = sb.tile([PARTS, 2, S], F32, name="u_second", tag="e_word_table")
         u = [u_first[:], u_second[:]]
         for t in range(2):
             nc.gpsimd.tensor_scalar(
-                u_first[:, t, :], a[:, t, :], c3[:, t : t + 1], c2[:, t : t + 1], ALU.mult, ALU.add
+                v_first[:, t, :], a[:, t, :], c1[:, t : t + 1], c0[:, t : t + 1], ALU.mult, ALU.add
             )
-        affine_on_scalar(v_first[:, 1, :], 1, slice(0, S), c1, c0)
+        affine_on_scalar(u_first[:, 1, :], 1, slice(0, S), c3, c2)
         for t in range(2, PACK):
             nc.vector.tensor_scalar(
                 u_second[:, t - 2, :], a[:, t, :], c3[:, t : t + 1], c2[:, t : t + 1], ALU.mult, ALU.add

@@ -145,10 +145,16 @@ def tile_picked_ylatt_lin_po_kernel(
         nc.vector.tensor_tensor(v_terms[:], along_a[:, :, :, 1], along_a[:, :, :, 0], ALU.add)
         nc.vector.tensor_tensor(u_terms[:], along_a[:, :, :, 1], along_a[:, :, :, 0], ALU.subtract)
         a = sb.tile([PARTS, PACK, S], F32, name="a")
-        for t in range(PACK):
+        for t in range(2):
             acc_a = ps.tile([PARTS, S], F32, name="acc_a%d" % t, tag="bank%d" % t)
             product(acc_a[:], "w1", t, x_picked[:], x_plane[:])
             nc.scalar.activation(a[:, t, :], acc_a[:], ACT.Tanh, scale=0.5)
+        for h in range(2):
+            cols = slice(h * HALF, (h + 1) * HALF)
+            acc_a = ps.tile([PARTS, 2, HALF], F32, name="acc_a%d" % (2 + h), tag="bank%d" % (2 + h))
+            for t in range(2, PACK):
+                product(acc_a[:, t - 2, :], "w1", t, x_picked[:, cols], x_plane[:, cols])
+            nc.scalar.activation(a[:, 2:PACK, cols], acc_a[:], ACT.Tanh, scale=0.5)
 
         for t0 in (0, 2):
             deal_weight(nc.vector.tensor_copy, "w2", w2_raw[:], 0, t0, t0 + 2)
@@ -183,7 +189,7 @@ def tile_picked_ylatt_lin_po_kernel(
             )
 
         v_first = placed.tile([PARTS, 2, S], F32, name="v_first", align_bytes=64, offset=2112)
-        u_second = sb.tile([PARTS, 2, S], F32, name="u_second", tag="e_word_table")
+        u_second = sb.tile([PARTS, 2, S], F32, name="u_second")
         u = [u_first[:], u_second[:]]
         for t in range(2):
             nc.gpsimd.tensor_scalar(

@@ -188,33 +188,35 @@ def tile_picked_ylatt_lin_po_kernel(
                 out, a[:, t, cols], ACT.Identity, bias=offset[:, t : t + 1], scale=factor[:, t : t + 1]
             )
 
-        v_first = placed.tile([PARTS, 2, S], F32, name="v_first", align_bytes=64, offset=2112)
+        v_first = placed.tile([PARTS, 1, S], F32, name="v_first", align_bytes=64, offset=4160)
         u_second = sb.tile([PARTS, 2, S], F32, name="u_second")
         u = [u_first[:], u_second[:]]
-        for t in range(2):
-            nc.gpsimd.tensor_scalar(
-                v_first[:, t, :], a[:, t, :], c1[:, t : t + 1], c0[:, t : t + 1], ALU.mult, ALU.add
-            )
+        nc.gpsimd.tensor_scalar(v_first[:, 0, :], a[:, 0, :], c1[:, 0:1], c0[:, 0:1], ALU.mult, ALU.add)
         affine_on_scalar(u_first[:, 1, :], 1, slice(0, S), c3, c2)
         for t in range(2, PACK):
             nc.vector.tensor_scalar(
                 u_second[:, t - 2, :], a[:, t, :], c3[:, t : t + 1], c2[:, t : t + 1], ALU.mult, ALU.add
             )
 
+        v_last = sb.tile([PARTS, 1, S], F32, name="v_last")
+        nc.vector.tensor_scalar(v_last[:, 0, :], a[:, 3, :], c1[:, 3:4], c0[:, 3:4], ALU.mult, ALU.add)
+
         v_second = []
         item_coordinate(stretches[0], (4, 5))
         for h, banks in ((0, (6, 7)), (1, (0, 1))):
             item_coordinate(stretches[h + 1], banks)
             v_half = placed.tile([PARTS, 2, HALF], F32, name="v_second%d" % h, align_bytes=64, offset=picked_at[h])
-            for t in range(2, PACK):
-                affine_on_scalar(v_half[:, t - 2, :], t, halves[h], c1, c0)
+            for t in range(1, 3):
+                affine_on_scalar(v_half[:, t - 1, :], t, halves[h], c1, c0)
             v_second.append(v_half)
 
         def v_part(t0, t1, cols):
-            if t0 < 2:
-                return v_first[:, t0:t1, cols]
+            if t0 == 0:
+                return v_first[:, :, cols]
+            if t0 == 3:
+                return v_last[:, :, cols]
             h = cols.start // HALF
-            return v_second[h][:, t0 - 2 : t1 - 2, cols.start - h * HALF : cols.stop - h * HALF]
+            return v_second[h][:, t0 - 1 : t1 - 1, cols.start - h * HALF : cols.stop - h * HALF]
 
         y_rows = out_0.rearrange("(p t) s -> p t s", t=PACK)
         y_words = out_1[0].rearrange("p c r -> p (c r)").bitcast(I32)
@@ -258,19 +260,21 @@ def tile_picked_ylatt_lin_po_kernel(
         for cols in stretches[:2]:
             for pair in range(2):
                 multiply(pair, cols)
-        add(0, 2, halves[0])
-        add(2, 4, halves[0])
+        add(0, 1, halves[0])
+        add(3, 4, halves[0])
+        add(1, 3, halves[0])
         store_rows(slice(0, PACK), halves[0])
         group_result(nc.scalar.copy, 0)
 
         for pair in range(2):
             multiply(pair, halves[1])
-        add(0, 2, halves[1])
-        store_rows(pairs[0], halves[1])
-        add(2, 4, chunks[1])
+        add(0, 1, halves[1])
+        add(3, 4, halves[1])
+        store_rows(slice(0, PACK, 3), halves[1])
+        add(1, 3, chunks[1])
         group_result(nc.scalar.copy, 1)
-        add(2, 4, chunks[2])
-        store_rows(pairs[1], halves[1])
+        add(1, 3, chunks[2])
+        store_rows(slice(1, 3), halves[1])
 
         quantize_result(0)
         store_words(halves[0])

from contextlib import ExitStack

import concourse.mybir as mybir

F32 = mybir.dt.float32
BF16 = mybir.dt.bfloat16
I32 = mybir.dt.int32
U32 = mybir.dt.uint32
U16 = mybir.dt.uint16
U8 = mybir.dt.uint8
FP8X4 = mybir.dt.float8_e4m3fn_x4
ALU = mybir.AluOpType
ACT = mybir.ActivationFunctionType

PARTS = 128
PACK = 4
K = 512
M = 512
S = 512
HALF = 256
QUARTER = 128
PER_COLUMN = 16
FLOPS = 2 * 2 * K * M * S

SCALAR_SHARE = 304

CHUNKS = ((0, 256), (256, 128), (384, 128))


def tile_picked_ylatt_lin_po_kernel(
    tc, x_words, x_scales, e_words, e_scales, w1, w2, theta, offs, item, out_0, out_1, out_2
):
    nc = tc.nc
    users = x_words.shape[2]
    items = e_words.shape[2]

    with ExitStack() as ctx:
        sb = ctx.enter_context(tc.tile_pool(name="sb", bufs=1))
        placed = ctx.enter_context(tc.tile_pool(name="placed", bufs=1))
        ps = ctx.enter_context(tc.psum_pool(name="ps", bufs=1))

        offs_sb = sb.tile([PARTS, S // PER_COLUMN], U16, name="offs_sb")
        item_sb = sb.tile([PARTS, S // PER_COLUMN], U16, name="item_sb")
        x_word_table = sb.tile([PARTS, users], I32, name="x_word_table")
        e_word_table = sb.tile([PARTS, items], I32, name="e_word_table", tag="e_word_table")
        x_scale_table = sb.tile([PARTS, users], U8, name="x_scale_table")
        e_scale_table = sb.tile([PARTS, items], U8, name="e_scale_table")
        theta_sb = sb.tile([PARTS, PACK, 4], F32, name="theta_sb")
        w1_raw = sb.tile([PARTS, PACK, M], F32, name="w1_raw", tag="w1_raw")
        w2_raw = sb.tile([PARTS, PACK, M], F32, name="w2_raw", tag="w2_raw")

        def load_words(table, words):
            nc.sync.dma_start(out=table[:], in_=words[0].rearrange("p c r -> p (c r)").bitcast(I32))

        def load_scales(table, scales, first):
            for r in range(4):
                nc.sync.dma_start(
                    out=table[first + r : PARTS : 32, :].bitcast(I32),
                    in_=scales[0, r:16:4, :].bitcast(I32),
                )

        nc.gpsimd.memset(x_scale_table[:].bitcast(I32), 0)
        nc.gpsimd.memset(e_scale_table[:].bitcast(I32), 0)
        e_plane = sb.tile([PARTS, S], U8, name="e_plane", align_bytes=64)
        nc.gpsimd.memset(e_plane[:].bitcast(I32), 0)

        nc.gpsimd.dma_start(out=theta_sb[:], in_=theta.rearrange("(p t) c -> p t c", t=PACK))
        load_words(x_word_table, x_words)
        nc.sync.dma_start(offs_sb[:], offs)
        load_scales(x_scale_table, x_scales, 0)
        nc.sync.dma_start(out=w1_raw[:], in_=w1.rearrange("(p j) m -> p j m", j=PACK))
        nc.sync.dma_start(item_sb[:], item)
        nc.sync.dma_start(out=e_scale_table[4:PARTS:8, :].bitcast(I32), in_=e_scales[0].bitcast(I32))
        nc.sync.dma_start(out=w2_raw[:], in_=w2.rearrange("(p j) m -> p j m", j=PACK))
        load_words(e_word_table, e_words)

        dealt = {}
        codes = {}
        planes = {}
        dealt["w1"] = sb.tile([PARTS, PACK, PARTS, PACK], BF16, name="w1_dealt", align_bytes=64)
        dealt["w2"] = placed.tile([PARTS, PACK, PARTS, PACK], BF16, name="w2_dealt", align_bytes=64, offset=6144)
        for w in ("w1", "w2"):
            codes[w] = sb.tile([PARTS, M], U32, name=w + "_codes", tag=w + "_codes", align_bytes=64)
            planes[w] = sb.tile([PARTS, M], U8, name=w + "_plane", align_bytes=64)

        def deal_weight(copy, w, raw, first_column, t0=0, t1=PACK):
            m0 = first_column // PACK
            copy(
                out=dealt[w][:, t0:t1, m0 : m0 + raw.shape[2] // PACK, :].rearrange("p t m j -> p m j t"),
                in_=raw.rearrange("p j (m t) -> p m j t", t=PACK)[:, :, :, t0:t1],
            )

        def quantize_weight(w, t0, t1):
            nc.vector.quantize_mx(
                out=codes[w][:, t0 * PARTS : t1 * PARTS].bitcast(FP8X4),
                scales=planes[w][:, t0 * PARTS : t1 * PARTS],
                in_=dealt[w][:, t0:t1, :, :].rearrange("p t m j -> p (t m j)"),
            )

        def product(acc, w, t, words, plane):
            nc.tensor.matmul_mx(
                out=acc,
                lhsT=codes[w][:, t * PARTS : (t + 1) * PARTS].bitcast(FP8X4),
                lhsT_scale=planes[w][:, t * PARTS : (t + 1) * PARTS],
                rhs=words.bitcast(FP8X4),
                rhs_scale=plane,
                start=True,
                stop=True,
            )

        x_picked = sb.tile([PARTS, S], U32, name="x_picked", align_bytes=64)
        x_plane = sb.tile([PARTS, S], U8, name="x_plane", align_bytes=64)
        nc.vector.tensor_copy(x_picked[:], x_word_table[:].bitcast(U32).indirect(offs_sb[:]))
        nc.vector.tensor_copy(x_plane[:], x_scale_table[:].indirect(offs_sb[:]))
        deal_weight(nc.scalar.copy, "w1", w1_raw[:, :, :SCALAR_SHARE], 0)
        nc.gpsimd.tensor_scalar(
            dealt["w1"][:, :, SCALAR_SHARE // PACK :, :].rearrange("p t m j -> p m t j"),
            w1_raw[:, :, SCALAR_SHARE:].rearrange("p j (m t) -> p m t j", t=PACK),
            1.0,
            0.0,
            ALU.mult,
            ALU.add,
        )
        e_rows = sb.tile([PARTS, S], U8, name="e_rows", align_bytes=64)
        nc.vector.tensor_copy(e_rows[:], e_scale_table[:].indirect(item_sb[:]))
        for r in range(4):
            nc.scalar.dma_start(
                out=e_plane[4 + r : PARTS : 32, :].bitcast(I32),
                in_=e_rows[4 + 8 * r : PARTS : 32, :].bitcast(I32),
            )
        quarter = sb.tile([PARTS, PACK, 2, 2], F32, name="quarter", tag="w1_raw")
        along_a = sb.tile([PARTS, 2, PACK, 2], F32, name="along_a")
        v_terms = sb.tile([PARTS, 2, PACK], F32, name="v_terms")
        u_terms = sb.tile([PARTS, 2, PACK], F32, name="u_terms")
        c0, c1 = v_terms[:, 0, :], v_terms[:, 1, :]
        c2, c3 = u_terms[:, 0, :], u_terms[:, 1, :]
        quantize_weight("w1", 0, 1)
        nc.vector.tensor_scalar(
            quarter[:].rearrange("p t b a -> p (t b a)"), theta_sb[:].rearrange("p t c -> p (t c)"), 0.25, None, ALU.mult
        )
        quantize_weight("w1", 1, 2)
        nc.vector.tensor_tensor(along_a[:, 0, :, :], quarter[:, :, :, 1], quarter[:, :, :, 0], ALU.add)
        nc.vector.tensor_tensor(along_a[:, 1, :, :], quarter[:, :, :, 1], quarter[:, :, :, 0], ALU.subtract)
        quantize_weight("w1", 2, PACK)
        nc.vector.tensor_tensor(v_terms[:], along_a[:, :, :, 1], along_a[:, :, :, 0], ALU.add)
        nc.vector.tensor_tensor(u_terms[:], along_a[:, :, :, 1], along_a[:, :, :, 0], ALU.subtract)
        a = sb.tile([PARTS, PACK, S], F32, name="a")
        for t in range(2):
            acc_a = ps.tile([PARTS, S], F32, name="acc_a%d" % t, tag="bank%d" % t)
            product(acc_a[:], "w1", t, x_picked[:], x_plane[:])
            nc.scalar.activation(a[:, t, :], acc_a[:], ACT.Tanh, scale=0.5)
        for h in range(2):
            cols = slice(h * HALF, (h + 1) * HALF)
            acc_a = ps.tile([PARTS, 2, HALF], F32, name="acc_a%d" % (2 + h), tag="bank%d" % (2 + h))
            for t in range(2, PACK):
                product(acc_a[:, t - 2, :], "w1", t, x_picked[:, cols], x_plane[:, cols])
            nc.scalar.activation(a[:, 2:PACK, cols], acc_a[:], ACT.Tanh, scale=0.5)

        for t0 in (0, 2):
            deal_weight(nc.vector.tensor_copy, "w2", w2_raw[:], 0, t0, t0 + 2)
        u_first = sb.tile([PARTS, 2, S], F32, name="u_first", tag="w2_raw")
        nc.vector.tensor_scalar(u_first[:, 0, :], a[:, 0, :], c3[:, 0:1], c2[:, 0:1], ALU.mult, ALU.add)
        for t0 in (0, 2):
            quantize_weight("w2", t0, t0 + 2)
        picked_at = (6208, 9280)
        e_picked = [
            placed.tile([PARTS, HALF], U32, name="e_picked%d" % h, align_bytes=64, offset=picked_at[h]) for h in range(2)
        ]
        stretches = [slice(0, QUARTER), slice(QUARTER, HALF), slice(HALF, S)]
        for h in range(2):
            offsets = item_sb[:, h * HALF // PER_COLUMN : (h + 1) * HALF // PER_COLUMN]
            nc.vector.tensor_copy(e_picked[h][:], e_word_table[:].bitcast(U32).indirect(offsets))
        p = sb.tile([PARTS, PACK, S], F32, name="p")

        halves = [slice(0, HALF), slice(HALF, S)]

        def item_coordinate(cols, banks):
            h = cols.start // HALF
            picked = e_picked[h][:, cols.start - h * HALF : cols.stop - h * HALF]
            for t0, bank in zip((0, 2), banks):
                acc_p = ps.tile([PARTS, 2, cols.stop - cols.start], F32, name="acc_p%d" % bank, tag="bank%d" % bank)
                for t in range(t0, t0 + 2):
                    product(acc_p[:, t - t0, :], "w2", t, picked, e_plane[4:, cols])
                nc.scalar.activation(p[:, t0 : t0 + 2, cols], acc_p[:], ACT.Tanh, scale=0.5)

        def affine_on_scalar(out, t, cols, factor, offset):
            nc.scalar.activation(
                out, a[:, t, cols], ACT.Identity, bias=offset[:, t : t + 1], scale=factor[:, t : t + 1]
            )

        v_first = placed.tile([PARTS, 1, S], F32, name="v_first", align_bytes=64, offset=4160)
        u_second = sb.tile([PARTS, 2, S], F32, name="u_second")
        u = [u_first[:], u_second[:]]
        nc.gpsimd.tensor_scalar(v_first[:, 0, :], a[:, 0, :], c1[:, 0:1], c0[:, 0:1], ALU.mult, ALU.add)
        affine_on_scalar(u_first[:, 1, :], 1, slice(0, S), c3, c2)
        for t in range(2, PACK):
            nc.vector.tensor_scalar(
                u_second[:, t - 2, :], a[:, t, :], c3[:, t : t + 1], c2[:, t : t + 1], ALU.mult, ALU.add
            )

        v_last = sb.tile([PARTS, 1, S], F32, name="v_last")
        nc.vector.tensor_scalar(v_last[:, 0, :], a[:, 3, :], c1[:, 3:4], c0[:, 3:4], ALU.mult, ALU.add)

        v_second = []
        item_coordinate(stretches[0], (4, 5))
        for h, banks in ((0, (6, 7)), (1, (0, 1))):
            item_coordinate(stretches[h + 1], banks)
            v_half = placed.tile([PARTS, 2, HALF], F32, name="v_second%d" % h, align_bytes=64, offset=picked_at[h])
            for t in range(1, 3):
                affine_on_scalar(v_half[:, t - 1, :], t, halves[h], c1, c0)
            v_second.append(v_half)

        def v_part(t0, t1, cols):
            if t0 == 0:
                return v_first[:, :, cols]
            if t0 == 3:
                return v_last[:, :, cols]
            h = cols.start // HALF
            return v_second[h][:, t0 - 1 : t1 - 1, cols.start - h * HALF : cols.stop - h * HALF]

        y_rows = out_0.rearrange("(p t) s -> p t s", t=PACK)
        y_words = out_1[0].rearrange("p c r -> p (c r)").bitcast(I32)
        up = sb.tile([PARTS, PACK, S], F32, name="up")
        y = sb.tile([PARTS, PACK, S], F32, name="y")
        y_grouped = [
            sb.tile([PARTS, width, PACK], BF16, name="y_grouped%d" % n, align_bytes=64)
            for n, (first, width) in enumerate(CHUNKS)
        ]
        y_codes = sb.tile([PARTS, S], U32, name="y_codes", align_bytes=64)
        y_plane = sb.tile([PARTS, S], U8, name="y_plane", align_bytes=64)
        pairs = [slice(0, 2), slice(2, 4)]
        chunks = [slice(first, first + width) for first, width in CHUNKS]

        def multiply(pair, cols):
            ts = pairs[pair]
            nc.vector.tensor_tensor(up[:, ts, cols], u[pair][:, :, cols], p[:, ts, cols], ALU.mult)

        def add(t0, t1, cols):
            nc.vector.tensor_tensor(y[:, t0:t1, cols], up[:, t0:t1, cols], v_part(t0, t1, cols), ALU.add)

        def store_rows(ts, cols):
            nc.sync.dma_start(out=y_rows[:, ts, cols], in_=y[:, ts, cols])

        def group_result(copy, n):
            copy(
                out=y_grouped[n][:].rearrange("p (c i) t -> p c t i", i=4),
                in_=y[:, :, chunks[n]].rearrange("p t (c i) -> p c t i", i=4),
            )

        def quantize_result(n):
            nc.vector.quantize_mx(
                out=y_codes[:, chunks[n]].bitcast(FP8X4),
                scales=y_plane[:, chunks[n]],
                in_=y_grouped[n][:].rearrange("p c t -> p (c t)"),
            )

        def store_words(cols):
            nc.sync.dma_start(out=y_words[:, cols], in_=y_codes[:, cols].bitcast(I32))

        for cols in stretches[:2]:
            for pair in range(2):
                multiply(pair, cols)
        add(0, 1, halves[0])
        add(3, 4, halves[0])
        add(1, 3, halves[0])
        store_rows(slice(0, PACK), halves[0])
        group_result(nc.scalar.copy, 0)

        for pair in range(2):
            multiply(pair, halves[1])
        add(0, 1, halves[1])
        add(3, 4, halves[1])
        store_rows(slice(0, PACK, 3), halves[1])
        add(1, 3, chunks[1])
        group_result(nc.scalar.copy, 1)
        add(1, 3, chunks[2])
        store_rows(slice(1, 3), halves[1])

        quantize_result(0)
        store_words(halves[0])
        group_result(nc.vector.tensor_copy, 2)
        quantize_result(1)
        quantize_result(2)
        store_words(halves[1])

        for q in range(4):
            queue = nc.scalar if q % 2 else nc.sync
            queue.dma_start(
                out=out_2[0, 4 * q : 4 * q + 4, :].bitcast(I32),
                in_=y_plane[32 * q : 32 * q + 4, :].bitcast(I32),
            )
